import numpy as np
import ml_dtypes


def mxq(x, axis, fmt="e4m3"):
    dtype, down = {"e4m3": (ml_dtypes.float8_e4m3fn, 7), "e5m2": (ml_dtypes.float8_e5m2, 14)}[fmt]
    v = np.moveaxis(np.asarray(x, np.float32).astype(ml_dtypes.bfloat16).astype(np.float64), axis, -1)
    blocks = v.reshape(v.shape[:-1] + (-1, 32))
    amax = np.abs(blocks).max(-1, keepdims=True)
    byte = np.maximum(np.where(amax > 0, np.frexp(amax)[1] - 1 + 127, 0) - down, 1)
    scale = np.exp2(byte - 127.0)
    codes = (blocks / scale).astype(np.float32).astype(dtype).astype(np.float64)
    return np.moveaxis((codes * scale).reshape(v.shape), -1, axis)


WIDE = False


def mx_kscale(k):
    if not WIDE:
        return np.ones(k)
    levels = np.array([18, -18])
    if k % 512:
        return np.exp2(np.random.permutation(np.resize(levels, k // 32))).repeat(32)
    a = np.empty((k // 512, 16))
    for p in range(k // 512):
        a[p, :8] = np.random.permutation(np.resize(levels, 8))
        for g in range(8):
            far = levels[np.abs(levels - a[p, g]) >= 10]
            a[p, g + 8] = far[np.random.randint(len(far))]
    return np.exp2(a.ravel()).repeat(32)


def f64(x):
    return np.asarray(x).astype(np.float64)


def striped(idx):
    return np.tile(np.asarray(idx).reshape(-1, 16).T, (8, 1)).astype(np.uint16)


def unstriped(offs):
    return offs[:16].T.reshape(-1).astype(np.int64)


B, N, T, D, R = 1, 512, 2048, 512, 1024


def setup_inputs():
    n = np.random.standard_normal
    idx = np.random.permutation(T)[:B * N]
    s = mx_kscale(D)[:, None]
    z = mx_kscale(R)[:, None]
    q = n((B, D, R))
    do = n((B, D, R))
    return {
        "qT": (q * s).astype(np.float32),
        "cT": (n((D, T)) * (0.50 / np.sqrt(D)) / s).astype(np.float32),
        "doT": (do * s).astype(np.float32),
        "rw": (np.random.uniform(0.5, 1.5, (B, R, 1)) * 1.0 / np.sqrt(R) * z).astype(np.float32),
        "qm": (q.transpose(0, 2, 1) / z).astype(np.float32),
        "dom": (do.transpose(0, 2, 1) / z).astype(np.float32),
        "offs": striped(idx),
    }


def reference(qT, cT, doT, rw, qm, dom, offs):
    idx = unstriped(offs)
    pick = lambda x: x[:, idx].reshape(x.shape[0], B, N).transpose(1, 0, 2)
    cq = mxq(pick(f64(cT)), 1, "e4m3")
    a = mxq(f64(qT), 1, "e4m3").transpose(0, 2, 1) @ cq
    p = np.exp(a)
    dp = mxq(f64(doT), 1, "e5m2").transpose(0, 2, 1) @ cq
    ds = f64(rw) * dp * p
    dk = mxq(f64(qm), 1, "e4m3").transpose(0, 2, 1) @ mxq(ds, 1, "e5m2")
    dv = mxq(f64(dom), 1, "e5m2").transpose(0, 2, 1) @ mxq(f64(rw) * p, 1, "e4m3")
    gc = np.zeros((D, T))
    gc[:, idx] = (dk + dv).transpose(1, 0, 2).reshape(D, B * N)
    return gc

@@ -1,0 +1,207 @@
+from contextlib import ExitStack
+
+import concourse.mybir as mybir
+
+N, T, D, R = 512, 2048, 512, 1024
+FLOPS = 4 * 2 * R * N * D
+
+F32 = mybir.dt.float32
+BF16 = mybir.dt.bfloat16
+U32 = mybir.dt.uint32
+U16 = mybir.dt.uint16
+U8 = mybir.dt.uint8
+E4M3 = mybir.dt.float8_e4m3fn_x4
+E5M2 = mybir.dt.float8_e5m2_x4
+MULT = mybir.AluOpType.mult
+EXP = mybir.ActivationFunctionType.Exp
+
+P = 128
+PACK = 4
+K_PASS = P * PACK
+GROUPS = R // K_PASS
+D_TILES = D // P
+HALF = K_PASS // 2
+M_LOADS = ((0, 1), (1, 2), (2, 4))
+
+
+def tile_attend_gat_exp_c_kernel(tc, qT, cT, doT, rw, qm, dom, offs, out):
+    nc = tc.nc
+
+    def copy_on(engine, dst, src):
+        if engine == "V":
+            nc.vector.tensor_copy(out=dst, in_=src)
+        else:
+            nc.scalar.copy(out=dst, in_=src)
+
+    with ExitStack() as ctx:
+        keep = ctx.enter_context(tc.tile_pool(name="keep", bufs=1))
+        ring = ctx.enter_context(tc.tile_pool(name="ring", bufs=2))
+        psum = ctx.enter_context(tc.psum_pool(name="psum", bufs=1))
+
+        def mx_tiles(name, width):
+            codes = keep.tile([P, width], U32, name=name + "_codes", align_bytes=64)
+            scales = keep.tile([P, width], U8, name=name + "_scales", align_bytes=64)
+            return codes, scales
+
+        def quantize(mx, fmt, src):
+            codes, scales = mx
+            nc.vector.quantize_mx(out=codes[:].bitcast(fmt), scales=scales[:], in_=src)
+
+        def matmul(dst, lhs, lhs_fmt, lhs_cols, rhs, rhs_fmt, start, stop):
+            nc.tensor.matmul_mx(
+                out=dst,
+                lhsT=lhs[0][:, lhs_cols].bitcast(lhs_fmt),
+                lhsT_scale=lhs[1][:, lhs_cols],
+                rhs=rhs[0][:].bitcast(rhs_fmt),
+                rhs_scale=rhs[1][:],
+                start=start,
+                stop=stop,
+            )
+
+        offsets = keep.tile([P, N // 16], U16, name="offsets")
+        nc.sync.dma_start(offsets[:], offs)
+        gates = keep.tile([P, GROUPS, PACK], F32, name="gates")
+        nc.scalar.dma_start(out=gates[:], in_=rw[0].rearrange("(g p t) o -> p g (t o)", g=GROUPS, t=PACK))
+
+        c_rows = cT.rearrange("(p j) x -> p j x", j=PACK)
+        planes = []
+        for j in range(PACK):
+            plane = keep.tile([P, T], F32, name="plane%d" % j)
+            nc.sync.dma_start(out=plane[:], in_=c_rows[:, j, :])
+            planes.append(plane)
+
+        left_raw = {}
+        for g in range(GROUPS):
+            for name, src in (("q", qT), ("do", doT)):
+                rows = src[0].rearrange("(p j) r -> p j r", j=PACK)
+                for h in range(2):
+                    raw = keep.tile([P, PACK, HALF], F32, name="%s_raw%d%d" % (name, g, h))
+                    r0 = g * K_PASS + h * HALF
+                    nc.sync.dma_start(out=raw[:], in_=rows[:, :, r0 : r0 + HALF])
+                    left_raw[name, g, h] = raw
+
+        right_raw = {}
+        for lo, hi in M_LOADS:
+            for name, src in (("dom", dom), ("qm", qm)):
+                for g in range(GROUPS):
+                    raw = keep.tile([P, PACK, (hi - lo) * P], F32, name="%s_raw%d%d" % (name, g, lo))
+                    rows = src[0, g * K_PASS : (g + 1) * K_PASS, :].rearrange("(p j) d -> p j d", j=PACK)
+                    nc.sync.dma_start(out=raw[:], in_=rows[:, :, lo * P : hi * P])
+                    for dt in range(lo, hi):
+                        right_raw[name, g, dt] = raw[:, :, (dt - lo) * P : (dt - lo + 1) * P]
+
+        windows = []
+        for dt in range(D_TILES):
+            window = keep.tile([P, T], F32, name="window%d" % dt)
+            nc.vector.memset(window[:], 0.0)
+            windows.append(window)
+
+        c_bf = keep.tile([P, N, PACK], BF16, name="c_bf", align_bytes=64)
+        for j in range(PACK):
+            nc.vector.tensor_copy(out=c_bf[:, :, j], in_=planes[j][:].indirect(offsets[:]))
+        c_mx = mx_tiles("c", N)
+        quantize(c_mx, E4M3, c_bf[:].rearrange("p i j -> p (i j)"))
+
+        left_mx = {}
+
+        def left_operand(name, g, fmt, engines):
+            bf = ring.tile([P, PACK, P, PACK], BF16, name="left_bf", align_bytes=64, bufs=3)
+            for h in range(2):
+                m = slice(h * (P // 2), (h + 1) * (P // 2))
+                copy_on(
+                    engines[h],
+                    bf[:, :, m, :].rearrange("p t m j -> p m j t"),
+                    left_raw[name, g, h][:].rearrange("p j (m t) -> p m j t", t=PACK),
+                )
+            mx = mx_tiles("%s%d" % (name, g), K_PASS)
+            quantize(mx, fmt, bf[:].rearrange("p t m j -> p (t m j)"))
+            left_mx[name, g] = mx
+
+        weights = {}
+
+        def scores(g):
+            p32 = keep.tile([P, PACK, N], F32, name="p32_%d" % g)
+            for t in range(PACK):
+                bank = psum.tile([P, N], F32, name="a_bank", bufs=3)
+                matmul(bank[:], left_mx["q", g], E4M3, slice(t * P, (t + 1) * P), c_mx, E4M3, True, True)
+                nc.scalar.activation(out=p32[:, t, :], in_=bank[:], func=EXP)
+            weights[g] = p32
+
+        moving = {}
+
+        def gated_weights(g):
+            bf = ring.tile([P, N, PACK], BF16, name="pw_bf", align_bytes=64)
+            nc.vector.tensor_tensor(
+                out=bf[:].rearrange("p (c i) t -> p c t i", i=4),
+                in0=weights[g][:].rearrange("p t (c i) -> p c t i", i=4),
+                in1=gates[:, g, :].unsqueeze(1).unsqueeze(3).to_broadcast([P, N // 4, PACK, 4]),
+                op=MULT,
+            )
+            return bf
+
+        def score_grads(g):
+            by_slot = ring.tile([P, PACK, N], BF16, name="ds_by_slot")
+            for t in range(PACK):
+                bank = psum.tile([P, N], F32, name="dp_bank", bufs=3)
+                matmul(bank[:], left_mx["do", g], E5M2, slice(t * P, (t + 1) * P), c_mx, E4M3, True, True)
+                nc.vector.scalar_tensor_tensor(
+                    out=by_slot[:, t, :], in0=bank[:], scalar=gates[:, g, t : t + 1], in1=weights[g][:, t, :], op0=MULT, op1=MULT
+                )
+            return by_slot
+
+        def interleave_grads(by_slot, shares):
+            bf = ring.tile([P, N, PACK], BF16, name="ds_bf", align_bytes=64)
+            for engine, lo, hi in shares:
+                copy_on(
+                    engine,
+                    bf[:, lo:hi, :].rearrange("p (c i) t -> p c t i", i=4),
+                    by_slot[:, :, lo:hi].rearrange("p t (c i) -> p c t i", i=4),
+                )
+            return bf
+
+        def quantize_moving(name, g, fmt, bf):
+            mx = mx_tiles("%s%d" % (name, g), N)
+            quantize(mx, fmt, bf[:].rearrange("p i t -> p (i t)"))
+            moving[name, g] = mx
+
+        def right_operand(name, dt, fmt):
+            bf = ring.tile([P, GROUPS, P, PACK], BF16, name="right_bf", align_bytes=64, bufs=4)
+            for g in range(GROUPS):
+                copy_on(
+                    "S",
+                    bf[:, g, :, :].rearrange("p (c i) j -> p c j i", i=4),
+                    right_raw[name, g, dt].rearrange("p j (c i) -> p c j i", i=4),
+                )
+            mx = mx_tiles("%s_t%d" % (name, dt), GROUPS * P)
+            quantize(mx, fmt, bf[:].rearrange("p g d j -> p (g d j)"))
+            return mx
+
+        def output_tile(dt, dom_mx, qm_mx):
+            bank = psum.tile([P, N], F32, name="out_bank", bufs=2)
+            for g in range(GROUPS):
+                cols = slice(g * P, (g + 1) * P)
+                matmul(bank[:], dom_mx, E5M2, cols, moving["pw", g], E4M3, g == 0, False)
+                matmul(bank[:], qm_mx, E4M3, cols, moving["ds", g], E5M2, False, g == GROUPS - 1)
+            sums = ring.tile([P, N], F32, name="sums")
+            nc.scalar.copy(out=sums[:], in_=bank[:])
+            nc.vector.tensor_copy(out=windows[dt][:].indirect(offsets[:]), in_=sums[:])
+            nc.sync.dma_start(out=out[dt * P : (dt + 1) * P, :], in_=windows[dt][:])
+
+        left_operand("q", 0, E4M3, "SV")
+        scores(0)
+        left_operand("do", 0, E5M2, "VV")
+        ds0 = score_grads(0)
+        left_operand("q", 1, E4M3, "SS")
+        pw0 = gated_weights(0)
+        scores(1)
+        left_operand("do", 1, E5M2, "SS")
+        quantize_moving("pw", 0, E4M3, pw0)
+        pw1 = gated_weights(1)
+        ds1 = score_grads(1)
+        quantize_moving("ds", 0, E5M2, interleave_grads(ds0, (("S", 0, N),)))
+        quantize_moving("pw", 1, E4M3, pw1)
+        right0 = (right_operand("dom", 0, E5M2), right_operand("qm", 0, E4M3))
+        quantize_moving("ds", 1, E5M2, interleave_grads(ds1, (("S", 0, 192), ("V", 192, N))))
+        output_tile(0, *right0)
+        for dt in range(1, D_TILES):
+            output_tile(dt, right_operand("dom", dt, E5M2), right_operand("qm", dt, E4M3))

@@ -21,6 +21,7 @@ K_PASS = P * PACK
 GROUPS = R // K_PASS
 D_TILES = D // P
 HALF = K_PASS // 2
+WINDOWS = 3
 M_LOADS = ((0, 1), (1, 2), (2, 4))
 
 
@@ -38,14 +39,14 @@ def tile_attend_gat_exp_c_kernel(tc, qT, cT, doT, rw, qm, dom, offs, out):
         ring = ctx.enter_context(tc.tile_pool(name="ring", bufs=2))
         psum = ctx.enter_context(tc.psum_pool(name="psum", bufs=1))
 
-        def mx_tiles(name, width):
-            codes = keep.tile([P, width], U32, name=name + "_codes", align_bytes=64)
+        def mx_tiles(name, width, tag=""):
+            codes = keep.tile([P, width], U32, name=name + "_codes", align_bytes=64, tag=tag)
             scales = keep.tile([P, width], U8, name=name + "_scales", align_bytes=64)
             return codes, scales
 
-        def quantize(mx, fmt, src):
+        def quantize(mx, fmt, src, cols=slice(None)):
             codes, scales = mx
-            nc.vector.quantize_mx(out=codes[:].bitcast(fmt), scales=scales[:], in_=src)
+            nc.vector.quantize_mx(out=codes[:, cols].bitcast(fmt), scales=scales[:, cols], in_=src)
 
         def matmul(dst, lhs, lhs_fmt, lhs_cols, rhs, rhs_fmt, start, stop):
             nc.tensor.matmul_mx(
@@ -91,7 +92,7 @@ def tile_attend_gat_exp_c_kernel(tc, qT, cT, doT, rw, qm, dom, offs, out):
                         right_raw[name, g, dt] = raw[:, :, (dt - lo) * P : (dt - lo + 1) * P]
 
         windows = []
-        for dt in range(D_TILES):
+        for dt in range(WINDOWS):
             window = keep.tile([P, T], F32, name="window%d" % dt)
             nc.vector.memset(window[:], 0.0)
             windows.append(window)
@@ -114,7 +115,8 @@ def tile_attend_gat_exp_c_kernel(tc, qT, cT, doT, rw, qm, dom, offs, out):
                     left_raw[name, g, h][:].rearrange("p j (m t) -> p m j t", t=PACK),
                 )
             mx = mx_tiles("%s%d" % (name, g), K_PASS)
-            quantize(mx, fmt, bf[:].rearrange("p t m j -> p (t m j)"))
+            for h in range(2):
+                quantize(mx, fmt, bf[:, 2 * h : 2 * h + 2].rearrange("p t m j -> p (t m j)"), slice(h * HALF, (h + 1) * HALF))
             left_mx[name, g] = mx
 
         weights = {}
@@ -131,12 +133,13 @@ def tile_attend_gat_exp_c_kernel(tc, qT, cT, doT, rw, qm, dom, offs, out):
 
         def gated_weights(g):
             bf = ring.tile([P, N, PACK], BF16, name="pw_bf", align_bytes=64)
-            nc.vector.tensor_tensor(
-                out=bf[:].rearrange("p (c i) t -> p c t i", i=4),
-                in0=weights[g][:].rearrange("p t (c i) -> p c t i", i=4),
-                in1=gates[:, g, :].unsqueeze(1).unsqueeze(3).to_broadcast([P, N // 4, PACK, 4]),
-                op=MULT,
-            )
+            for lo in (0, N // 2):
+                nc.vector.tensor_tensor(
+                    out=bf[:, lo : lo + N // 2, :].rearrange("p (c i) t -> p c t i", i=4),
+                    in0=weights[g][:, :, lo : lo + N // 2].rearrange("p t (c i) -> p c t i", i=4),
+                    in1=gates[:, g, :].unsqueeze(1).unsqueeze(3).to_broadcast([P, N // 8, PACK, 4]),
+                    op=MULT,
+                )
             return bf
 
         def score_grads(g):
@@ -149,13 +152,14 @@ def tile_attend_gat_exp_c_kernel(tc, qT, cT, doT, rw, qm, dom, offs, out):
                 )
             return by_slot
 
-        def interleave_grads(by_slot, shares):
+        def interleave_grads(by_slot, engines):
             bf = ring.tile([P, N, PACK], BF16, name="ds_bf", align_bytes=64)
-            for engine, lo, hi in shares:
+            for n, engine in enumerate(engines):
+                cols = slice(n * P, (n + 1) * P)
                 copy_on(
                     engine,
-                    bf[:, lo:hi, :].rearrange("p (c i) t -> p c t i", i=4),
-                    by_slot[:, :, lo:hi].rearrange("p t (c i) -> p c t i", i=4),
+                    bf[:, cols, :].rearrange("p (c i) t -> p c t i", i=4),
+                    by_slot[:, :, cols].rearrange("p t (c i) -> p c t i", i=4),
                 )
             return bf
 
@@ -164,17 +168,24 @@ def tile_attend_gat_exp_c_kernel(tc, qT, cT, doT, rw, qm, dom, offs, out):
             quantize(mx, fmt, bf[:].rearrange("p i t -> p (i t)"))
             moving[name, g] = mx
 
-        def right_operand(name, dt, fmt):
-            bf = ring.tile([P, GROUPS, P, PACK], BF16, name="right_bf", align_bytes=64, bufs=4)
-            for g in range(GROUPS):
-                copy_on(
-                    "S",
-                    bf[:, g, :, :].rearrange("p (c i) j -> p c j i", i=4),
-                    right_raw[name, g, dt].rearrange("p j (c i) -> p c j i", i=4),
-                )
-            mx = mx_tiles("%s_t%d" % (name, dt), GROUPS * P)
-            quantize(mx, fmt, bf[:].rearrange("p g d j -> p (g d j)"))
-            return mx
+        def right_copies(dt, engines):
+            tag = "late%d" % (dt - 2) if dt >= 2 else ""
+            bf = keep.tile([P, 2, GROUPS, P, PACK], BF16, name="right_bf%d" % dt, align_bytes=64, tag=tag)
+            for n, name in enumerate(("dom", "qm")):
+                for g in range(GROUPS):
+                    copy_on(
+                        engines[n],
+                        bf[:, n, g, :, :].rearrange("p (c i) j -> p c j i", i=4),
+                        right_raw[name, g, dt].rearrange("p j (c i) -> p c j i", i=4),
+                    )
+            return bf
+
+        def right_operands(dt, bf):
+            dom_mx = mx_tiles("dom_t%d" % dt, GROUPS * P)
+            qm_mx = mx_tiles("qm_t%d" % dt, GROUPS * P, tag="late%d" % dt if dt < 2 else "")
+            quantize(dom_mx, E5M2, bf[:, 0].rearrange("p g d j -> p (g d j)"))
+            quantize(qm_mx, E4M3, bf[:, 1].rearrange("p g d j -> p (g d j)"))
+            return dom_mx, qm_mx
 
         def output_tile(dt, dom_mx, qm_mx):
             bank = psum.tile([P, N], F32, name="out_bank", bufs=2)
@@ -184,24 +195,30 @@ def tile_attend_gat_exp_c_kernel(tc, qT, cT, doT, rw, qm, dom, offs, out):
                 matmul(bank[:], qm_mx, E4M3, cols, moving["ds", g], E5M2, False, g == GROUPS - 1)
             sums = ring.tile([P, N], F32, name="sums")
             nc.scalar.copy(out=sums[:], in_=bank[:])
-            nc.vector.tensor_copy(out=windows[dt][:].indirect(offsets[:]), in_=sums[:])
-            nc.sync.dma_start(out=out[dt * P : (dt + 1) * P, :], in_=windows[dt][:])
+            nc.vector.tensor_copy(out=windows[dt % WINDOWS][:].indirect(offsets[:]), in_=sums[:])
+            nc.sync.dma_start(out=out[dt * P : (dt + 1) * P, :], in_=windows[dt % WINDOWS][:])
 
         left_operand("q", 0, E4M3, "SV")
         scores(0)
-        left_operand("do", 0, E5M2, "VV")
+        left_operand("do", 0, E5M2, "SV")
+        left_operand("q", 1, E4M3, "VS")
         ds0 = score_grads(0)
-        left_operand("q", 1, E4M3, "SS")
-        pw0 = gated_weights(0)
-        scores(1)
         left_operand("do", 1, E5M2, "SS")
-        quantize_moving("pw", 0, E4M3, pw0)
-        pw1 = gated_weights(1)
+        scores(1)
         ds1 = score_grads(1)
-        quantize_moving("ds", 0, E5M2, interleave_grads(ds0, (("S", 0, N),)))
+        ds0 = interleave_grads(ds0, "SSSS")
+        bf0 = right_copies(0, "SS")
+        ds1 = interleave_grads(ds1, "SSSV")
+        quantize_moving("pw", 0, E4M3, gated_weights(0))
+        pw1 = gated_weights(1)
+        quantize_moving("ds", 0, E5M2, ds0)
+        right0 = right_operands(0, bf0)
         quantize_moving("pw", 1, E4M3, pw1)
-        right0 = (right_operand("dom", 0, E5M2), right_operand("qm", 0, E4M3))
-        quantize_moving("ds", 1, E5M2, interleave_grads(ds1, (("S", 0, 192), ("V", 192, N))))
+        quantize_moving("ds", 1, E5M2, ds1)
+        right1 = right_operands(1, right_copies(1, "VS"))
         output_tile(0, *right0)
-        for dt in range(1, D_TILES):
-            output_tile(dt, right_operand("dom", dt, E5M2), right_operand("qm", dt, E4M3))
+        right2 = right_operands(2, right_copies(2, "SS"))
+        output_tile(1, *right1)
+        right3 = right_operands(3, right_copies(3, "SS"))
+        output_tile(2, *right2)
+        output_tile(3, *right3)

@@ -1,6 +1,7 @@
 from contextlib import ExitStack
 
 import concourse.mybir as mybir
+from concourse.masks import make_identity
 
 N, T, D, R = 512, 2048, 512, 1024
 FLOPS = 4 * 2 * R * N * D
@@ -13,6 +14,7 @@ U8 = mybir.dt.uint8
 E4M3 = mybir.dt.float8_e4m3fn_x4
 E5M2 = mybir.dt.float8_e5m2_x4
 MULT = mybir.AluOpType.mult
+ADD = mybir.AluOpType.add
 EXP = mybir.ActivationFunctionType.Exp
 
 P = 128
@@ -31,6 +33,8 @@ def tile_attend_gat_exp_c_kernel(tc, qT, cT, doT, rw, qm, dom, offs, out):
     def copy_on(engine, dst, src):
         if engine == "V":
             nc.vector.tensor_copy(out=dst, in_=src)
+        elif engine == "G":
+            nc.gpsimd.tensor_scalar(out=dst, in0=src, scalar1=1.0, scalar2=0.0, op0=MULT, op1=ADD)
         else:
             nc.scalar.copy(out=dst, in_=src)
 
@@ -61,8 +65,20 @@ def tile_attend_gat_exp_c_kernel(tc, qT, cT, doT, rw, qm, dom, offs, out):
 
         offsets = keep.tile([P, N // 16], U16, name="offsets")
         nc.sync.dma_start(offsets[:], offs)
+        padded = keep.tile([P, P], F32, name="padded")
+        nc.vector.memset(padded[:], 0.0)
         gates = keep.tile([P, GROUPS, PACK], F32, name="gates")
         nc.scalar.dma_start(out=gates[:], in_=rw[0].rearrange("(g p t) o -> p g (t o)", g=GROUPS, t=PACK))
+        nc.vector.tensor_copy(out=padded[:, : GROUPS * PACK], in_=gates[:].rearrange("p g t -> p (g t)"))
+        identity = keep.tile([P, P], F32, name="identity")
+        make_identity(nc, identity[:])
+        turned_bank = psum.tile([P, P], F32, name="out_bank", tag="a_out", bufs=4)
+        nc.tensor.transpose(turned_bank[:], padded[:], identity[:])
+        turned = keep.tile([P, P], F32, name="turned")
+        nc.scalar.copy(out=turned[:], in_=turned_bank[:])
+        gate_bank = psum.tile([P, P], F32, name="gate_bank")
+        nc.tensor.transpose(gate_bank[:], turned[:], identity[:])
+        bank_gates = gate_bank[:, : GROUPS * PACK].rearrange("p (g t) -> p g t", t=PACK)
 
         c_rows = cT.rearrange("(p j) x -> p j x", j=PACK)
         planes = []
@@ -94,7 +110,7 @@ def tile_attend_gat_exp_c_kernel(tc, qT, cT, doT, rw, qm, dom, offs, out):
         windows = []
         for dt in range(WINDOWS):
             window = keep.tile([P, T], F32, name="window%d" % dt)
-            nc.vector.memset(window[:], 0.0)
+            nc.gpsimd.memset(window[:], 0.0)
             windows.append(window)
 
         c_bf = keep.tile([P, N, PACK], BF16, name="c_bf", align_bytes=64)
@@ -105,15 +121,20 @@ def tile_attend_gat_exp_c_kernel(tc, qT, cT, doT, rw, qm, dom, offs, out):
 
         left_mx = {}
 
-        def left_operand(name, g, fmt, engines):
-            bf = ring.tile([P, PACK, P, PACK], BF16, name="left_bf", align_bytes=64, bufs=3)
-            for h in range(2):
-                m = slice(h * (P // 2), (h + 1) * (P // 2))
-                copy_on(
-                    engines[h],
-                    bf[:, :, m, :].rearrange("p t m j -> p m j t"),
-                    left_raw[name, g, h][:].rearrange("p j (m t) -> p m j t", t=PACK),
-                )
+        left_bf = {}
+
+        def left_cast(name, g, h, engine):
+            if (name, g) not in left_bf:
+                left_bf[name, g] = keep.tile([P, PACK, P, PACK], BF16, name="left_bf", align_bytes=64, tag="left_%s%d" % (name, g))
+            m = slice(h * (P // 2), (h + 1) * (P // 2))
+            copy_on(
+                engine,
+                left_bf[name, g][:, :, m, :].rearrange("p t m j -> p m j t"),
+                left_raw[name, g, h][:].rearrange("p j (m t) -> p m j t", t=PACK),
+            )
+
+        def left_quantize(name, g, fmt):
+            bf = left_bf[name, g]
             mx = mx_tiles("%s%d" % (name, g), K_PASS)
             for h in range(2):
                 quantize(mx, fmt, bf[:, 2 * h : 2 * h + 2].rearrange("p t m j -> p (t m j)"), slice(h * HALF, (h + 1) * HALF))
@@ -122,25 +143,40 @@ def tile_attend_gat_exp_c_kernel(tc, qT, cT, doT, rw, qm, dom, offs, out):
         weights = {}
 
         def scores(g):
-            p32 = keep.tile([P, PACK, N], F32, name="p32_%d" % g)
+            p32 = keep.tile([P, PACK, N], F32, name="p32_%d" % g, align_bytes=64)
             for t in range(PACK):
-                bank = psum.tile([P, N], F32, name="a_bank", bufs=3)
+                bank = psum.tile([P, N], F32, name="a_bank", tag="a_out", bufs=4)
                 matmul(bank[:], left_mx["q", g], E4M3, slice(t * P, (t + 1) * P), c_mx, E4M3, True, True)
                 nc.scalar.activation(out=p32[:, t, :], in_=bank[:], func=EXP)
             weights[g] = p32
 
         moving = {}
 
-        def gated_weights(g):
-            bf = ring.tile([P, N, PACK], BF16, name="pw_bf", align_bytes=64)
-            for lo in (0, N // 2):
+        def gated_half(g, half, engine, tag=""):
+            bf = keep.tile([P, N // 2, PACK], BF16, name="pw_bf%d%d" % (g, half), align_bytes=64, tag=tag)
+            first = half * (N // 2)
+            if engine == "V":
                 nc.vector.tensor_tensor(
-                    out=bf[:, lo : lo + N // 2, :].rearrange("p (c i) t -> p c t i", i=4),
-                    in0=weights[g][:, :, lo : lo + N // 2].rearrange("p t (c i) -> p c t i", i=4),
-                    in1=gates[:, g, :].unsqueeze(1).unsqueeze(3).to_broadcast([P, N // 8, PACK, 4]),
+                    out=bf[:].rearrange("p (c i) t -> p c t i", i=4),
+                    in0=weights[g][:, :, first : first + N // 2].rearrange("p t (c i) -> p c t i", i=4),
+                    in1=bank_gates[:, g, :].unsqueeze(1).unsqueeze(3).to_broadcast([P, N // 8, PACK, 4]),
                     op=MULT,
                 )
+            else:
+                for lo in (0, P):
+                    nc.gpsimd.tensor_tensor(
+                        out=bf[:, lo : lo + P, :],
+                        in0=weights[g][:, :, first + lo : first + lo + P].rearrange("p t i -> p i t"),
+                        in1=gates[:, g, :].unsqueeze(1).to_broadcast([P, P, PACK]),
+                        op=MULT,
+                    )
             return bf
+
+        def quantize_halves(name, g, fmt, halves):
+            mx = mx_tiles("%s%d" % (name, g), N)
+            for h, bf in enumerate(halves):
+                quantize(mx, fmt, bf[:].rearrange("p i t -> p (i t)"), slice(h * HALF, (h + 1) * HALF))
+            moving[name, g] = mx
 
         def score_grads(g):
             by_slot = ring.tile([P, PACK, N], BF16, name="ds_by_slot")
@@ -168,13 +204,13 @@ def tile_attend_gat_exp_c_kernel(tc, qT, cT, doT, rw, qm, dom, offs, out):
             quantize(mx, fmt, bf[:].rearrange("p i t -> p (i t)"))
             moving[name, g] = mx
 
-        def right_copies(dt, engines):
-            tag = "late%d" % (dt - 2) if dt >= 2 else ""
+        def right_copies(dt, engines, tag=""):
+            tag = "late%d" % (dt - 2) if dt >= 2 else tag
             bf = keep.tile([P, 2, GROUPS, P, PACK], BF16, name="right_bf%d" % dt, align_bytes=64, tag=tag)
             for n, name in enumerate(("dom", "qm")):
                 for g in range(GROUPS):
                     copy_on(
-                        engines[n],
+                        engines[2 * n + g],
                         bf[:, n, g, :, :].rearrange("p (c i) j -> p c j i", i=4),
                         right_raw[name, g, dt].rearrange("p j (c i) -> p c j i", i=4),
                     )
@@ -188,7 +224,7 @@ def tile_attend_gat_exp_c_kernel(tc, qT, cT, doT, rw, qm, dom, offs, out):
             return dom_mx, qm_mx
 
         def output_tile(dt, dom_mx, qm_mx):
-            bank = psum.tile([P, N], F32, name="out_bank", bufs=2)
+            bank = psum.tile([P, N], F32, name="out_bank", tag="a_out", bufs=4)
             for g in range(GROUPS):
                 cols = slice(g * P, (g + 1) * P)
                 matmul(bank[:], dom_mx, E5M2, cols, moving["pw", g], E4M3, g == 0, False)
@@ -198,27 +234,38 @@ def tile_attend_gat_exp_c_kernel(tc, qT, cT, doT, rw, qm, dom, offs, out):
             nc.vector.tensor_copy(out=windows[dt % WINDOWS][:].indirect(offsets[:]), in_=sums[:])
             nc.sync.dma_start(out=out[dt * P : (dt + 1) * P, :], in_=windows[dt % WINDOWS][:])
 
-        left_operand("q", 0, E4M3, "SV")
+        left_cast("q", 0, 0, "S")
+        left_cast("q", 0, 1, "V")
+        left_quantize("q", 0, E4M3)
         scores(0)
-        left_operand("do", 0, E5M2, "SV")
-        left_operand("q", 1, E4M3, "VS")
+        left_cast("do", 0, 0, "V")
+        left_cast("do", 0, 1, "V")
+        left_quantize("do", 0, E5M2)
+        left_cast("q", 1, 0, "V")
         ds0 = score_grads(0)
-        left_operand("do", 1, E5M2, "SS")
+        pw0a = gated_half(0, 0, "G")
+        left_cast("q", 1, 1, "S")
+        left_quantize("q", 1, E4M3)
+        left_cast("do", 1, 0, "S")
         scores(1)
+        left_cast("do", 1, 1, "V")
+        left_quantize("do", 1, E5M2)
         ds1 = score_grads(1)
+        pw0b = gated_half(0, 1, "G", "left_do1")
         ds0 = interleave_grads(ds0, "SSSS")
-        bf0 = right_copies(0, "SS")
-        ds1 = interleave_grads(ds1, "SSSV")
-        quantize_moving("pw", 0, E4M3, gated_weights(0))
-        pw1 = gated_weights(1)
+        bf0 = right_copies(0, "GGGS", "p32_0")
+        ds1 = interleave_grads(ds1, "SSSS")
+        pw1a = gated_half(1, 0, "V")
+        pw1b = gated_half(1, 1, "V")
         quantize_moving("ds", 0, E5M2, ds0)
         right0 = right_operands(0, bf0)
-        quantize_moving("pw", 1, E4M3, pw1)
+        quantize_halves("pw", 0, E4M3, (pw0a, pw0b))
+        quantize_halves("pw", 1, E4M3, (pw1a, pw1b))
         quantize_moving("ds", 1, E5M2, ds1)
-        right1 = right_operands(1, right_copies(1, "VS"))
+        right1 = right_operands(1, right_copies(1, "SSSS", ""))
         output_tile(0, *right0)
-        right2 = right_operands(2, right_copies(2, "SS"))
+        right2 = right_operands(2, right_copies(2, "SSSS"))
         output_tile(1, *right1)
-        right3 = right_operands(3, right_copies(3, "SS"))
+        right3 = right_operands(3, right_copies(3, "SSSS"))
         output_tile(2, *right2)
         output_tile(3, *right3)

@@ -100,12 +100,12 @@ def tile_attend_gat_exp_c_kernel(tc, qT, cT, doT, rw, qm, dom, offs, out):
         right_raw = {}
         for lo, hi in M_LOADS:
             for name, src in (("dom", dom), ("qm", qm)):
+                raw = keep.tile([P, GROUPS, PACK, (hi - lo) * P], F32, name="%s_raw%d" % (name, lo))
                 for g in range(GROUPS):
-                    raw = keep.tile([P, PACK, (hi - lo) * P], F32, name="%s_raw%d%d" % (name, g, lo))
                     rows = src[0, g * K_PASS : (g + 1) * K_PASS, :].rearrange("(p j) d -> p j d", j=PACK)
-                    nc.sync.dma_start(out=raw[:], in_=rows[:, :, lo * P : hi * P])
-                    for dt in range(lo, hi):
-                        right_raw[name, g, dt] = raw[:, :, (dt - lo) * P : (dt - lo + 1) * P]
+                    nc.sync.dma_start(out=raw[:, g], in_=rows[:, :, lo * P : hi * P])
+                for dt in range(lo, hi):
+                    right_raw[name, dt] = raw[:, :, :, (dt - lo) * P : (dt - lo + 1) * P]
 
         windows = []
         for dt in range(WINDOWS):
@@ -123,9 +123,9 @@ def tile_attend_gat_exp_c_kernel(tc, qT, cT, doT, rw, qm, dom, offs, out):
 
         left_bf = {}
 
-        def left_cast(name, g, h, engine):
+        def left_cast(name, g, h, engine, tag=""):
             if (name, g) not in left_bf:
-                left_bf[name, g] = keep.tile([P, PACK, P, PACK], BF16, name="left_bf", align_bytes=64, tag="left_%s%d" % (name, g))
+                left_bf[name, g] = keep.tile([P, PACK, P, PACK], BF16, name="left_bf", align_bytes=64, tag=tag or "left_%s%d" % (name, g))
             m = slice(h * (P // 2), (h + 1) * (P // 2))
             copy_on(
                 engine,
@@ -152,31 +152,23 @@ def tile_attend_gat_exp_c_kernel(tc, qT, cT, doT, rw, qm, dom, offs, out):
 
         moving = {}
 
-        def gated_half(g, half, engine, tag=""):
-            bf = keep.tile([P, N // 2, PACK], BF16, name="pw_bf%d%d" % (g, half), align_bytes=64, tag=tag)
-            first = half * (N // 2)
-            if engine == "V":
-                nc.vector.tensor_tensor(
-                    out=bf[:].rearrange("p (c i) t -> p c t i", i=4),
-                    in0=weights[g][:, :, first : first + N // 2].rearrange("p t (c i) -> p c t i", i=4),
-                    in1=bank_gates[:, g, :].unsqueeze(1).unsqueeze(3).to_broadcast([P, N // 8, PACK, 4]),
-                    op=MULT,
-                )
-            else:
-                for lo in (0, P):
-                    nc.gpsimd.tensor_tensor(
-                        out=bf[:, lo : lo + P, :],
-                        in0=weights[g][:, :, first + lo : first + lo + P].rearrange("p t i -> p i t"),
-                        in1=gates[:, g, :].unsqueeze(1).to_broadcast([P, P, PACK]),
-                        op=MULT,
-                    )
-            return bf
+        def gated_on_gpsimd(g, bf, slots):
+            width = slots.stop - slots.start
+            nc.gpsimd.tensor_tensor(
+                out=bf[:, slots, :],
+                in0=weights[g][:, :, slots].rearrange("p t i -> p i t"),
+                in1=gates[:, g, :].unsqueeze(1).to_broadcast([P, width, PACK]),
+                op=MULT,
+            )
 
-        def quantize_halves(name, g, fmt, halves):
-            mx = mx_tiles("%s%d" % (name, g), N)
-            for h, bf in enumerate(halves):
-                quantize(mx, fmt, bf[:].rearrange("p i t -> p (i t)"), slice(h * HALF, (h + 1) * HALF))
-            moving[name, g] = mx
+        def gated_on_vector(g, bf, slots):
+            width = slots.stop - slots.start
+            nc.vector.tensor_tensor(
+                out=bf[:, slots, :].rearrange("p (c i) t -> p c t i", i=4),
+                in0=weights[g][:, :, slots].rearrange("p t (c i) -> p c t i", i=4),
+                in1=bank_gates[:, g, :].unsqueeze(1).unsqueeze(3).to_broadcast([P, width // 4, PACK, 4]),
+                op=MULT,
+            )
 
         def score_grads(g):
             by_slot = ring.tile([P, PACK, N], BF16, name="ds_by_slot")
@@ -191,7 +183,7 @@ def tile_attend_gat_exp_c_kernel(tc, qT, cT, doT, rw, qm, dom, offs, out):
         def interleave_grads(by_slot, engines):
             bf = ring.tile([P, N, PACK], BF16, name="ds_bf", align_bytes=64)
             for n, engine in enumerate(engines):
-                cols = slice(n * P, (n + 1) * P)
+                cols = slice(n * N // len(engines), (n + 1) * N // len(engines))
                 copy_on(
                     engine,
                     bf[:, cols, :].rearrange("p (c i) t -> p c t i", i=4),
@@ -199,8 +191,8 @@ def tile_attend_gat_exp_c_kernel(tc, qT, cT, doT, rw, qm, dom, offs, out):
                 )
             return bf
 
-        def quantize_moving(name, g, fmt, bf):
-            mx = mx_tiles("%s%d" % (name, g), N)
+        def quantize_moving(name, g, fmt, bf, tag=""):
+            mx = mx_tiles("%s%d" % (name, g), N, tag)
             quantize(mx, fmt, bf[:].rearrange("p i t -> p (i t)"))
             moving[name, g] = mx
 
@@ -208,11 +200,18 @@ def tile_attend_gat_exp_c_kernel(tc, qT, cT, doT, rw, qm, dom, offs, out):
             tag = "late%d" % (dt - 2) if dt >= 2 else tag
             bf = keep.tile([P, 2, GROUPS, P, PACK], BF16, name="right_bf%d" % dt, align_bytes=64, tag=tag)
             for n, name in enumerate(("dom", "qm")):
+                if engines[2 * n : 2 * n + 2] == "SS":
+                    copy_on(
+                        "S",
+                        bf[:, n].rearrange("p g (c i) j -> p g c j i", i=4),
+                        right_raw[name, dt].rearrange("p g j (c i) -> p g c j i", i=4),
+                    )
+                    continue
                 for g in range(GROUPS):
                     copy_on(
                         engines[2 * n + g],
                         bf[:, n, g, :, :].rearrange("p (c i) j -> p c j i", i=4),
-                        right_raw[name, g, dt].rearrange("p j (c i) -> p c j i", i=4),
+                        right_raw[name, dt][:, g].rearrange("p j (c i) -> p c j i", i=4),
                     )
             return bf
 
@@ -238,31 +237,34 @@ def tile_attend_gat_exp_c_kernel(tc, qT, cT, doT, rw, qm, dom, offs, out):
         left_cast("q", 0, 1, "V")
         left_quantize("q", 0, E4M3)
         scores(0)
-        left_cast("do", 0, 0, "V")
+        left_cast("do", 0, 0, "V", "left_q0")
         left_cast("do", 0, 1, "V")
         left_quantize("do", 0, E5M2)
-        left_cast("q", 1, 0, "V")
         ds0 = score_grads(0)
-        pw0a = gated_half(0, 0, "G")
+        pw0 = keep.tile([P, N, PACK], BF16, name="pw0_bf", align_bytes=64, tag="left_q0")
+        gated_on_gpsimd(0, pw0, slice(0, 256))
+        left_cast("q", 1, 0, "S")
         left_cast("q", 1, 1, "S")
         left_quantize("q", 1, E4M3)
         left_cast("do", 1, 0, "S")
-        scores(1)
+        gated_on_vector(0, pw0, slice(256, N))
         left_cast("do", 1, 1, "V")
+        scores(1)
         left_quantize("do", 1, E5M2)
+        quantize_moving("pw", 0, E4M3, pw0, "left_do1")
         ds1 = score_grads(1)
-        pw0b = gated_half(0, 1, "G", "left_do1")
+        bf0 = right_copies(0, "GGGS", "left_q0")
         ds0 = interleave_grads(ds0, "SSSS")
-        bf0 = right_copies(0, "GGGS", "p32_0")
-        ds1 = interleave_grads(ds1, "SSSS")
-        pw1a = gated_half(1, 0, "V")
-        pw1b = gated_half(1, 1, "V")
-        quantize_moving("ds", 0, E5M2, ds0)
+        ds1 = interleave_grads(ds1, "SS")
+        pw1 = keep.tile([P, N, PACK], BF16, name="pw1_bf", align_bytes=64, tag="do1_codes")
+        gated_on_gpsimd(1, pw1, slice(0, 128))
+        gated_on_vector(1, pw1, slice(128, N))
+        bf1 = right_copies(1, "SSSS")
+        quantize_moving("ds", 0, E5M2, ds0, "p32_1")
         right0 = right_operands(0, bf0)
-        quantize_halves("pw", 0, E4M3, (pw0a, pw0b))
-        quantize_halves("pw", 1, E4M3, (pw1a, pw1b))
+        quantize_moving("pw", 1, E4M3, pw1)
         quantize_moving("ds", 1, E5M2, ds1)
-        right1 = right_operands(1, right_copies(1, "SSSS", ""))
+        right1 = right_operands(1, bf1)
         output_tile(0, *right0)
         right2 = right_operands(2, right_copies(2, "SSSS"))
         output_tile(1, *right1)

@@ -72,7 +72,7 @@ def tile_attend_gat_exp_c_kernel(tc, qT, cT, doT, rw, qm, dom, offs, out):
         nc.vector.tensor_copy(out=padded[:, : GROUPS * PACK], in_=gates[:].rearrange("p g t -> p (g t)"))
         identity = keep.tile([P, P], F32, name="identity")
         make_identity(nc, identity[:])
-        turned_bank = psum.tile([P, P], F32, name="out_bank", tag="a_out", bufs=4)
+        turned_bank = psum.tile([P, P], F32, name="out_bank", tag="dp_out", bufs=3)
         nc.tensor.transpose(turned_bank[:], padded[:], identity[:])
         turned = keep.tile([P, P], F32, name="turned")
         nc.scalar.copy(out=turned[:], in_=turned_bank[:])
@@ -142,20 +142,20 @@ def tile_attend_gat_exp_c_kernel(tc, qT, cT, doT, rw, qm, dom, offs, out):
 
         weights = {}
 
-        def scores(g):
-            p32 = keep.tile([P, PACK, N], F32, name="p32_%d" % g, align_bytes=64)
-            for t in range(PACK):
-                bank = psum.tile([P, N], F32, name="a_bank", tag="a_out", bufs=4)
+        def scores(g, places=range(PACK)):
+            if g not in weights:
+                weights[g] = keep.tile([P, PACK, N], F32, name="p32_%d" % g, align_bytes=64)
+            for t in places:
+                bank = psum.tile([P, N], F32, name="a_bank", bufs=4)
                 matmul(bank[:], left_mx["q", g], E4M3, slice(t * P, (t + 1) * P), c_mx, E4M3, True, True)
-                nc.scalar.activation(out=p32[:, t, :], in_=bank[:], func=EXP)
-            weights[g] = p32
+                nc.scalar.activation(out=weights[g][:, t, :], in_=bank[:], func=EXP)
 
         moving = {}
 
         def gated_on_gpsimd(g, bf, slots):
             width = slots.stop - slots.start
             nc.gpsimd.tensor_tensor(
-                out=bf[:, slots, :],
+                out=bf,
                 in0=weights[g][:, :, slots].rearrange("p t i -> p i t"),
                 in1=gates[:, g, :].unsqueeze(1).to_broadcast([P, width, PACK]),
                 op=MULT,
@@ -164,70 +164,71 @@ def tile_attend_gat_exp_c_kernel(tc, qT, cT, doT, rw, qm, dom, offs, out):
         def gated_on_vector(g, bf, slots):
             width = slots.stop - slots.start
             nc.vector.tensor_tensor(
-                out=bf[:, slots, :].rearrange("p (c i) t -> p c t i", i=4),
+                out=bf.rearrange("p (c i) t -> p c t i", i=4),
                 in0=weights[g][:, :, slots].rearrange("p t (c i) -> p c t i", i=4),
                 in1=bank_gates[:, g, :].unsqueeze(1).unsqueeze(3).to_broadcast([P, width // 4, PACK, 4]),
                 op=MULT,
             )
 
-        def score_grads(g):
-            by_slot = ring.tile([P, PACK, N], BF16, name="ds_by_slot")
-            for t in range(PACK):
-                bank = psum.tile([P, N], F32, name="dp_bank", bufs=3)
+        def quantize_half(name, g, fmt, h, bf, tag=""):
+            if h == 0:
+                moving[name, g] = mx_tiles("%s%d" % (name, g), N, tag)
+            quantize(moving[name, g], fmt, bf[:].rearrange("p i t -> p (i t)"), slice(h * HALF, (h + 1) * HALF))
+
+        def score_grads(g, places=range(PACK), by_slot=None):
+            if by_slot is None:
+                by_slot = ring.tile([P, PACK, N], BF16, name="ds_by_slot")
+            for t in places:
+                bank = psum.tile([P, N], F32, name="dp_bank", tag="dp_out", bufs=3)
                 matmul(bank[:], left_mx["do", g], E5M2, slice(t * P, (t + 1) * P), c_mx, E4M3, True, True)
                 nc.vector.scalar_tensor_tensor(
                     out=by_slot[:, t, :], in0=bank[:], scalar=gates[:, g, t : t + 1], in1=weights[g][:, t, :], op0=MULT, op1=MULT
                 )
             return by_slot
 
-        def interleave_grads(by_slot, engines):
-            bf = ring.tile([P, N, PACK], BF16, name="ds_bf", align_bytes=64)
-            for n, engine in enumerate(engines):
-                cols = slice(n * N // len(engines), (n + 1) * N // len(engines))
-                copy_on(
-                    engine,
-                    bf[:, cols, :].rearrange("p (c i) t -> p c t i", i=4),
-                    by_slot[:, :, cols].rearrange("p t (c i) -> p c t i", i=4),
-                )
-            return bf
+        def interleave_grads(bf, by_slot, engine, slots):
+            copy_on(
+                engine,
+                bf[:, slots, :].rearrange("p (c i) t -> p c t i", i=4),
+                by_slot[:, :, slots].rearrange("p t (c i) -> p c t i", i=4),
+            )
 
         def quantize_moving(name, g, fmt, bf, tag=""):
             mx = mx_tiles("%s%d" % (name, g), N, tag)
             quantize(mx, fmt, bf[:].rearrange("p i t -> p (i t)"))
             moving[name, g] = mx
 
-        def right_copies(dt, engines, tag=""):
-            tag = "late%d" % (dt - 2) if dt >= 2 else tag
-            bf = keep.tile([P, 2, GROUPS, P, PACK], BF16, name="right_bf%d" % dt, align_bytes=64, tag=tag)
-            for n, name in enumerate(("dom", "qm")):
-                if engines[2 * n : 2 * n + 2] == "SS":
-                    copy_on(
-                        "S",
-                        bf[:, n].rearrange("p g (c i) j -> p g c j i", i=4),
-                        right_raw[name, dt].rearrange("p g j (c i) -> p g c j i", i=4),
-                    )
-                    continue
-                for g in range(GROUPS):
-                    copy_on(
-                        engines[2 * n + g],
-                        bf[:, n, g, :, :].rearrange("p (c i) j -> p c j i", i=4),
-                        right_raw[name, dt][:, g].rearrange("p j (c i) -> p c j i", i=4),
-                    )
+        def right_cast(name, dt, engine, tag=""):
+            bf = keep.tile([P, GROUPS, P, PACK], BF16, name="%s_bf%d" % (name, dt), align_bytes=64, tag=tag)
+            copy_on(
+                engine,
+                bf[:].rearrange("p g (c i) j -> p g c j i", i=4),
+                right_raw[name, dt].rearrange("p g j (c i) -> p g c j i", i=4),
+            )
             return bf
 
-        def right_operands(dt, bf):
-            dom_mx = mx_tiles("dom_t%d" % dt, GROUPS * P)
-            qm_mx = mx_tiles("qm_t%d" % dt, GROUPS * P, tag="late%d" % dt if dt < 2 else "")
-            quantize(dom_mx, E5M2, bf[:, 0].rearrange("p g d j -> p (g d j)"))
-            quantize(qm_mx, E4M3, bf[:, 1].rearrange("p g d j -> p (g d j)"))
-            return dom_mx, qm_mx
+        def right_quantize(name, dt, fmt, bf, tag=""):
+            mx = mx_tiles("%s_t%d" % (name, dt), GROUPS * P, tag)
+            quantize(mx, fmt, bf[:].rearrange("p g d j -> p (g d j)"))
+            return mx
+
+        def late_operands(dt):
+            bf = keep.tile([P, 2, GROUPS, P, PACK], BF16, name="late_bf%d" % dt, align_bytes=64, tag=("p32_1", "qm_t1_codes")[dt - 2])
+            for n, name in enumerate(("dom", "qm")):
+                copy_on(
+                    "S",
+                    bf[:, n].rearrange("p g (c i) j -> p g c j i", i=4),
+                    right_raw[name, dt].rearrange("p g j (c i) -> p g c j i", i=4),
+                )
+            return right_quantize("dom", dt, E5M2, bf[:, 0]), right_quantize("qm", dt, E4M3, bf[:, 1])
 
         def output_tile(dt, dom_mx, qm_mx):
-            bank = psum.tile([P, N], F32, name="out_bank", tag="a_out", bufs=4)
-            for g in range(GROUPS):
-                cols = slice(g * P, (g + 1) * P)
-                matmul(bank[:], dom_mx, E5M2, cols, moving["pw", g], E4M3, g == 0, False)
-                matmul(bank[:], qm_mx, E4M3, cols, moving["ds", g], E5M2, False, g == GROUPS - 1)
+            bank = psum.tile([P, N], F32, name="out_bank", tag="dp_out", bufs=3)
+            first, second = slice(0, P), slice(P, 2 * P)
+            matmul(bank[:], qm_mx, E4M3, first, moving["ds", 0], E5M2, True, False)
+            matmul(bank[:], dom_mx, E5M2, first, moving["pw", 0], E4M3, False, False)
+            matmul(bank[:], dom_mx, E5M2, second, moving["pw", 1], E4M3, False, False)
+            matmul(bank[:], qm_mx, E4M3, second, moving["ds", 1], E5M2, False, True)
             sums = ring.tile([P, N], F32, name="sums")
             nc.scalar.copy(out=sums[:], in_=bank[:])
             nc.vector.tensor_copy(out=windows[dt % WINDOWS][:].indirect(offsets[:]), in_=sums[:])
@@ -241,33 +242,43 @@ def tile_attend_gat_exp_c_kernel(tc, qT, cT, doT, rw, qm, dom, offs, out):
         left_cast("do", 0, 1, "V")
         left_quantize("do", 0, E5M2)
         ds0 = score_grads(0)
-        pw0 = keep.tile([P, N, PACK], BF16, name="pw0_bf", align_bytes=64, tag="left_q0")
-        gated_on_gpsimd(0, pw0, slice(0, 256))
+        pw0a = keep.tile([P, HALF, PACK], BF16, name="pw0a_bf", align_bytes=64, tag="left_q0")
+        gated_on_gpsimd(0, pw0a[:], slice(0, HALF))
         left_cast("q", 1, 0, "S")
         left_cast("q", 1, 1, "S")
         left_quantize("q", 1, E4M3)
         left_cast("do", 1, 0, "S")
-        gated_on_vector(0, pw0, slice(256, N))
-        left_cast("do", 1, 1, "V")
         scores(1)
+        left_cast("do", 1, 1, "V")
         left_quantize("do", 1, E5M2)
-        quantize_moving("pw", 0, E4M3, pw0, "left_do1")
+        ds0_bf = keep.tile([P, N, PACK], BF16, name="ds0_bf", align_bytes=64, tag="left_q1")
+        interleave_grads(ds0_bf, ds0, "V", slice(0, 256))
+        quantize_half("pw", 0, E4M3, 0, pw0a, "left_do1")
         ds1 = score_grads(1)
-        bf0 = right_copies(0, "GGGS", "left_q0")
-        ds0 = interleave_grads(ds0, "SSSS")
-        ds1 = interleave_grads(ds1, "SS")
+        pw0b = keep.tile([P, HALF, PACK], BF16, name="pw0b_bf", align_bytes=64, tag="left_q0")
+        gated_on_gpsimd(0, pw0b[:], slice(HALF, N))
+        interleave_grads(ds0_bf, ds0, "S", slice(256, N))
+        dom0 = right_cast("dom", 0, "S")
+        qm0 = right_cast("qm", 0, "S")
+        ds1_bf = keep.tile([P, N, PACK], BF16, name="ds1_bf", align_bytes=64)
+        interleave_grads(ds1_bf, ds1, "S", slice(0, HALF))
+        interleave_grads(ds1_bf, ds1, "S", slice(HALF, N))
         pw1 = keep.tile([P, N, PACK], BF16, name="pw1_bf", align_bytes=64, tag="do1_codes")
-        gated_on_gpsimd(1, pw1, slice(0, 128))
-        gated_on_vector(1, pw1, slice(128, N))
-        bf1 = right_copies(1, "SSSS")
-        quantize_moving("ds", 0, E5M2, ds0, "p32_1")
-        right0 = right_operands(0, bf0)
+        gated_on_gpsimd(1, pw1[:, :160], slice(0, 160))
+        gated_on_vector(1, pw1[:, 160:], slice(160, N))
+        qm0 = right_quantize("qm", 0, E4M3, qm0, "p32_1")
+        quantize_moving("ds", 0, E5M2, ds0_bf, "p32_0")
+        dom0 = right_quantize("dom", 0, E5M2, dom0, "")
+        quantize_half("pw", 0, E4M3, 1, pw0b)
         quantize_moving("pw", 1, E4M3, pw1)
-        quantize_moving("ds", 1, E5M2, ds1)
-        right1 = right_operands(1, bf1)
-        output_tile(0, *right0)
-        right2 = right_operands(2, right_copies(2, "SSSS"))
-        output_tile(1, *right1)
-        right3 = right_operands(3, right_copies(3, "SSSS"))
+        quantize_moving("ds", 1, E5M2, ds1_bf)
+        qm1 = right_cast("qm", 1, "S")
+        dom1 = right_cast("dom", 1, "V", "do1_codes")
+        qm1 = right_quantize("qm", 1, E4M3, qm1)
+        dom1 = right_quantize("dom", 1, E5M2, dom1)
+        output_tile(0, dom0, qm0)
+        right2 = late_operands(2)
+        output_tile(1, dom1, qm1)
+        right3 = late_operands(3)
         output_tile(2, *right2)
         output_tile(3, *right3)

@@ -114,10 +114,15 @@ def tile_attend_gat_exp_c_kernel(tc, qT, cT, doT, rw, qm, dom, offs, out):
             windows.append(window)
 
         c_bf = keep.tile([P, N, PACK], BF16, name="c_bf", align_bytes=64)
-        for j in range(PACK):
+        for j in range(PACK - 1):
             nc.vector.tensor_copy(out=c_bf[:, :, j], in_=planes[j][:].indirect(offsets[:]))
+        for h in range(2):
+            listed = offsets[:, h * HALF // 16 : (h + 1) * HALF // 16]
+            nc.vector.tensor_copy(out=c_bf[:, h * HALF : (h + 1) * HALF, PACK - 1], in_=planes[PACK - 1][:].indirect(listed))
         c_mx = mx_tiles("c", N)
-        quantize(c_mx, E4M3, c_bf[:].rearrange("p i j -> p (i j)"))
+        for h in range(2):
+            cols = slice(h * HALF, (h + 1) * HALF)
+            quantize(c_mx, E4M3, c_bf[:, cols, :].rearrange("p i j -> p (i j)"), cols)
 
         left_mx = {}
 
@@ -127,17 +132,19 @@ def tile_attend_gat_exp_c_kernel(tc, qT, cT, doT, rw, qm, dom, offs, out):
             if (name, g) not in left_bf:
                 left_bf[name, g] = keep.tile([P, PACK, P, PACK], BF16, name="left_bf", align_bytes=64, tag=tag or "left_%s%d" % (name, g))
             m = slice(h * (P // 2), (h + 1) * (P // 2))
-            copy_on(
-                engine,
-                left_bf[name, g][:, :, m, :].rearrange("p t m j -> p m j t"),
-                left_raw[name, g, h][:].rearrange("p j (m t) -> p m j t", t=PACK),
-            )
+            dst = left_bf[name, g][:, :, m, :].rearrange("p t m j -> p m j t")
+            src = left_raw[name, g, h][:].rearrange("p j (m t) -> p m j t", t=PACK)
+            if engine == "V" and h == 1:
+                for lo in (0, 2):
+                    copy_on(engine, dst[:, :, :, lo : lo + 2], src[:, :, :, lo : lo + 2])
+            else:
+                copy_on(engine, dst, src)
 
         def left_quantize(name, g, fmt):
             bf = left_bf[name, g]
             mx = mx_tiles("%s%d" % (name, g), K_PASS)
-            for h in range(2):
-                quantize(mx, fmt, bf[:, 2 * h : 2 * h + 2].rearrange("p t m j -> p (t m j)"), slice(h * HALF, (h + 1) * HALF))
+            for lo, hi in ((0, 1), (1, 2), (2, PACK)):
+                quantize(mx, fmt, bf[:, lo:hi].rearrange("p t m j -> p (t m j)"), slice(lo * P, hi * P))
             left_mx[name, g] = mx
 
         weights = {}
@@ -213,7 +220,7 @@ def tile_attend_gat_exp_c_kernel(tc, qT, cT, doT, rw, qm, dom, offs, out):
             return mx
 
         def late_operands(dt):
-            bf = keep.tile([P, 2, GROUPS, P, PACK], BF16, name="late_bf%d" % dt, align_bytes=64, tag=("p32_1", "qm_t1_codes")[dt - 2])
+            bf = keep.tile([P, 2, GROUPS, P, PACK], BF16, name="late_bf%d" % dt, align_bytes=64, tag=("p32_0", "qm_t1_codes")[dt - 2])
             for n, name in enumerate(("dom", "qm")):
                 copy_on(
                     "S",
@@ -238,11 +245,11 @@ def tile_attend_gat_exp_c_kernel(tc, qT, cT, doT, rw, qm, dom, offs, out):
         left_cast("q", 0, 1, "V")
         left_quantize("q", 0, E4M3)
         scores(0)
-        left_cast("do", 0, 0, "V", "left_q0")
+        left_cast("do", 0, 0, "V")
         left_cast("do", 0, 1, "V")
         left_quantize("do", 0, E5M2)
         ds0 = score_grads(0)
-        pw0a = keep.tile([P, HALF, PACK], BF16, name="pw0a_bf", align_bytes=64, tag="left_q0")
+        pw0a = keep.tile([P, HALF, PACK], BF16, name="pw0a_bf", align_bytes=64, tag="left_do0")
         gated_on_gpsimd(0, pw0a[:], slice(0, HALF))
         left_cast("q", 1, 0, "S")
         left_cast("q", 1, 1, "S")
@@ -255,7 +262,7 @@ def tile_attend_gat_exp_c_kernel(tc, qT, cT, doT, rw, qm, dom, offs, out):
         interleave_grads(ds0_bf, ds0, "V", slice(0, 256))
         quantize_half("pw", 0, E4M3, 0, pw0a, "left_do1")
         ds1 = score_grads(1)
-        pw0b = keep.tile([P, HALF, PACK], BF16, name="pw0b_bf", align_bytes=64, tag="left_q0")
+        pw0b = keep.tile([P, HALF, PACK], BF16, name="pw0b_bf", align_bytes=64, tag="left_do0")
         gated_on_gpsimd(0, pw0b[:], slice(HALF, N))
         interleave_grads(ds0_bf, ds0, "S", slice(256, N))
         dom0 = right_cast("dom", 0, "S")
@@ -264,10 +271,10 @@ def tile_attend_gat_exp_c_kernel(tc, qT, cT, doT, rw, qm, dom, offs, out):
         interleave_grads(ds1_bf, ds1, "S", slice(0, HALF))
         interleave_grads(ds1_bf, ds1, "S", slice(HALF, N))
         pw1 = keep.tile([P, N, PACK], BF16, name="pw1_bf", align_bytes=64, tag="do1_codes")
-        gated_on_gpsimd(1, pw1[:, :160], slice(0, 160))
-        gated_on_vector(1, pw1[:, 160:], slice(160, N))
-        qm0 = right_quantize("qm", 0, E4M3, qm0, "p32_1")
-        quantize_moving("ds", 0, E5M2, ds0_bf, "p32_0")
+        gated_on_gpsimd(1, pw1[:, :128], slice(0, 128))
+        gated_on_vector(1, pw1[:, 128:], slice(128, N))
+        qm0 = right_quantize("qm", 0, E4M3, qm0, "p32_0")
+        quantize_moving("ds", 0, E5M2, ds0_bf, "c_codes")
         dom0 = right_quantize("dom", 0, E5M2, dom0, "")
         quantize_half("pw", 0, E4M3, 1, pw0b)
         quantize_moving("pw", 1, E4M3, pw1)

@@ -72,7 +72,7 @@ def tile_attend_gat_exp_c_kernel(tc, qT, cT, doT, rw, qm, dom, offs, out):
         nc.vector.tensor_copy(out=padded[:, : GROUPS * PACK], in_=gates[:].rearrange("p g t -> p (g t)"))
         identity = keep.tile([P, P], F32, name="identity")
         make_identity(nc, identity[:])
-        turned_bank = psum.tile([P, P], F32, name="out_bank", tag="dp_out", bufs=3)
+        turned_bank = psum.tile([P, P], F32, name="out_bank", tag="work", bufs=7)
         nc.tensor.transpose(turned_bank[:], padded[:], identity[:])
         turned = keep.tile([P, P], F32, name="turned")
         nc.scalar.copy(out=turned[:], in_=turned_bank[:])
@@ -140,12 +140,12 @@ def tile_attend_gat_exp_c_kernel(tc, qT, cT, doT, rw, qm, dom, offs, out):
             else:
                 copy_on(engine, dst, src)
 
-        def left_quantize(name, g, fmt):
+        def left_quantize(name, g, fmt, runs=((0, 1), (1, 2), (2, PACK))):
             bf = left_bf[name, g]
-            mx = mx_tiles("%s%d" % (name, g), K_PASS)
-            for lo, hi in ((0, 1), (1, 2), (2, PACK)):
-                quantize(mx, fmt, bf[:, lo:hi].rearrange("p t m j -> p (t m j)"), slice(lo * P, hi * P))
-            left_mx[name, g] = mx
+            if (name, g) not in left_mx:
+                left_mx[name, g] = mx_tiles("%s%d" % (name, g), K_PASS)
+            for lo, hi in runs:
+                quantize(left_mx[name, g], fmt, bf[:, lo:hi].rearrange("p t m j -> p (t m j)"), slice(lo * P, hi * P))
 
         weights = {}
 
@@ -153,7 +153,7 @@ def tile_attend_gat_exp_c_kernel(tc, qT, cT, doT, rw, qm, dom, offs, out):
             if g not in weights:
                 weights[g] = keep.tile([P, PACK, N], F32, name="p32_%d" % g, align_bytes=64)
             for t in places:
-                bank = psum.tile([P, N], F32, name="a_bank", bufs=4)
+                bank = psum.tile([P, N], F32, name="a_bank", tag="work", bufs=7)
                 matmul(bank[:], left_mx["q", g], E4M3, slice(t * P, (t + 1) * P), c_mx, E4M3, True, True)
                 nc.scalar.activation(out=weights[g][:, t, :], in_=bank[:], func=EXP)
 
@@ -186,7 +186,7 @@ def tile_attend_gat_exp_c_kernel(tc, qT, cT, doT, rw, qm, dom, offs, out):
             if by_slot is None:
                 by_slot = ring.tile([P, PACK, N], BF16, name="ds_by_slot")
             for t in places:
-                bank = psum.tile([P, N], F32, name="dp_bank", tag="dp_out", bufs=3)
+                bank = psum.tile([P, N], F32, name="dp_bank", tag="work", bufs=7)
                 matmul(bank[:], left_mx["do", g], E5M2, slice(t * P, (t + 1) * P), c_mx, E4M3, True, True)
                 nc.vector.scalar_tensor_tensor(
                     out=by_slot[:, t, :], in0=bank[:], scalar=gates[:, g, t : t + 1], in1=weights[g][:, t, :], op0=MULT, op1=MULT
@@ -196,7 +196,7 @@ def tile_attend_gat_exp_c_kernel(tc, qT, cT, doT, rw, qm, dom, offs, out):
         def interleave_grads(bf, by_slot, engine, slots):
             copy_on(
                 engine,
-                bf[:, slots, :].rearrange("p (c i) t -> p c t i", i=4),
+                bf.rearrange("p (c i) t -> p c t i", i=4),
                 by_slot[:, :, slots].rearrange("p t (c i) -> p c t i", i=4),
             )
 
@@ -219,23 +219,19 @@ def tile_attend_gat_exp_c_kernel(tc, qT, cT, doT, rw, qm, dom, offs, out):
             quantize(mx, fmt, bf[:].rearrange("p g d j -> p (g d j)"))
             return mx
 
-        def late_operands(dt):
-            bf = keep.tile([P, 2, GROUPS, P, PACK], BF16, name="late_bf%d" % dt, align_bytes=64, tag=("p32_0", "qm_t1_codes")[dt - 2])
-            for n, name in enumerate(("dom", "qm")):
-                copy_on(
-                    "S",
-                    bf[:, n].rearrange("p g (c i) j -> p g c j i", i=4),
-                    right_raw[name, dt].rearrange("p g j (c i) -> p g c j i", i=4),
-                )
-            return right_quantize("dom", dt, E5M2, bf[:, 0]), right_quantize("qm", dt, E4M3, bf[:, 1])
-
         def output_tile(dt, dom_mx, qm_mx):
-            bank = psum.tile([P, N], F32, name="out_bank", tag="dp_out", bufs=3)
+            bank = psum.tile([P, N], F32, name="out_bank", tag="work", bufs=7)
             first, second = slice(0, P), slice(P, 2 * P)
-            matmul(bank[:], qm_mx, E4M3, first, moving["ds", 0], E5M2, True, False)
-            matmul(bank[:], dom_mx, E5M2, first, moving["pw", 0], E4M3, False, False)
-            matmul(bank[:], dom_mx, E5M2, second, moving["pw", 1], E4M3, False, False)
-            matmul(bank[:], qm_mx, E4M3, second, moving["ds", 1], E5M2, False, True)
+            passes = [
+                (qm_mx, E4M3, first, moving["ds", 0], E5M2),
+                (dom_mx, E5M2, first, moving["pw", 0], E4M3),
+                (dom_mx, E5M2, second, moving["pw", 1], E4M3),
+                (qm_mx, E4M3, second, moving["ds", 1], E5M2),
+            ]
+            if dt >= 2:
+                passes = passes[1:3] + passes[:1] + passes[3:]
+            for n, operands in enumerate(passes):
+                matmul(bank[:], *operands, n == 0, n == len(passes) - 1)
             sums = ring.tile([P, N], F32, name="sums")
             nc.scalar.copy(out=sums[:], in_=bank[:])
             nc.vector.tensor_copy(out=windows[dt % WINDOWS][:].indirect(offsets[:]), in_=sums[:])
@@ -255,26 +251,28 @@ def tile_attend_gat_exp_c_kernel(tc, qT, cT, doT, rw, qm, dom, offs, out):
         left_cast("q", 1, 1, "S")
         left_quantize("q", 1, E4M3)
         left_cast("do", 1, 0, "S")
+        ds0b = keep.tile([P, HALF, PACK], BF16, name="ds0b_bf", align_bytes=64)
+        interleave_grads(ds0b[:], ds0, "S", slice(HALF, N))
         scores(1)
         left_cast("do", 1, 1, "V")
         left_quantize("do", 1, E5M2)
-        ds0_bf = keep.tile([P, N, PACK], BF16, name="ds0_bf", align_bytes=64, tag="left_q1")
-        interleave_grads(ds0_bf, ds0, "V", slice(0, 256))
+        ds0a = keep.tile([P, HALF, PACK], BF16, name="ds0a_bf", align_bytes=64, tag="left_q1")
+        interleave_grads(ds0a[:], ds0, "V", slice(0, HALF))
         quantize_half("pw", 0, E4M3, 0, pw0a, "left_do1")
         ds1 = score_grads(1)
         pw0b = keep.tile([P, HALF, PACK], BF16, name="pw0b_bf", align_bytes=64, tag="left_do0")
         gated_on_gpsimd(0, pw0b[:], slice(HALF, N))
-        interleave_grads(ds0_bf, ds0, "S", slice(256, N))
         dom0 = right_cast("dom", 0, "S")
         qm0 = right_cast("qm", 0, "S")
         ds1_bf = keep.tile([P, N, PACK], BF16, name="ds1_bf", align_bytes=64)
-        interleave_grads(ds1_bf, ds1, "S", slice(0, HALF))
-        interleave_grads(ds1_bf, ds1, "S", slice(HALF, N))
+        interleave_grads(ds1_bf[:, :HALF], ds1, "S", slice(0, HALF))
+        interleave_grads(ds1_bf[:, HALF:], ds1, "S", slice(HALF, N))
         pw1 = keep.tile([P, N, PACK], BF16, name="pw1_bf", align_bytes=64, tag="do1_codes")
         gated_on_gpsimd(1, pw1[:, :128], slice(0, 128))
         gated_on_vector(1, pw1[:, 128:], slice(128, N))
         qm0 = right_quantize("qm", 0, E4M3, qm0, "p32_0")
-        quantize_moving("ds", 0, E5M2, ds0_bf, "c_codes")
+        quantize_half("ds", 0, E5M2, 0, ds0a, "c_codes")
+        quantize_half("ds", 0, E5M2, 1, ds0b)
         dom0 = right_quantize("dom", 0, E5M2, dom0, "")
         quantize_half("pw", 0, E4M3, 1, pw0b)
         quantize_moving("pw", 1, E4M3, pw1)
@@ -283,9 +281,15 @@ def tile_attend_gat_exp_c_kernel(tc, qT, cT, doT, rw, qm, dom, offs, out):
         dom1 = right_cast("dom", 1, "V", "do1_codes")
         qm1 = right_quantize("qm", 1, E4M3, qm1)
         dom1 = right_quantize("dom", 1, E5M2, dom1)
+        dom2 = right_cast("dom", 2, "S", "")
         output_tile(0, dom0, qm0)
-        right2 = late_operands(2)
+        dom2 = right_quantize("dom", 2, E5M2, dom2)
+        qm2 = right_cast("qm", 2, "S", "p32_0")
+        dom3 = right_cast("dom", 3, "S", "dom_t0_codes")
+        qm2 = right_quantize("qm", 2, E4M3, qm2)
+        dom3 = right_quantize("dom", 3, E5M2, dom3)
         output_tile(1, dom1, qm1)
-        right3 = late_operands(3)
-        output_tile(2, *right2)
-        output_tile(3, *right3)
+        qm3 = right_cast("qm", 3, "S", "qm_t1_codes")
+        qm3 = right_quantize("qm", 3, E4M3, qm3)
+        output_tile(2, dom2, qm2)
+        output_tile(3, dom3, qm3)

@@ -72,7 +72,7 @@ def tile_attend_gat_exp_c_kernel(tc, qT, cT, doT, rw, qm, dom, offs, out):
         nc.vector.tensor_copy(out=padded[:, : GROUPS * PACK], in_=gates[:].rearrange("p g t -> p (g t)"))
         identity = keep.tile([P, P], F32, name="identity")
         make_identity(nc, identity[:])
-        turned_bank = psum.tile([P, P], F32, name="out_bank", tag="work", bufs=7)
+        turned_bank = psum.tile([P, P], F32, name="out_bank", tag="dp_out", bufs=3)
         nc.tensor.transpose(turned_bank[:], padded[:], identity[:])
         turned = keep.tile([P, P], F32, name="turned")
         nc.scalar.copy(out=turned[:], in_=turned_bank[:])
@@ -153,7 +153,7 @@ def tile_attend_gat_exp_c_kernel(tc, qT, cT, doT, rw, qm, dom, offs, out):
             if g not in weights:
                 weights[g] = keep.tile([P, PACK, N], F32, name="p32_%d" % g, align_bytes=64)
             for t in places:
-                bank = psum.tile([P, N], F32, name="a_bank", tag="work", bufs=7)
+                bank = psum.tile([P, N], F32, name="a_bank", bufs=4)
                 matmul(bank[:], left_mx["q", g], E4M3, slice(t * P, (t + 1) * P), c_mx, E4M3, True, True)
                 nc.scalar.activation(out=weights[g][:, t, :], in_=bank[:], func=EXP)
 
@@ -186,7 +186,7 @@ def tile_attend_gat_exp_c_kernel(tc, qT, cT, doT, rw, qm, dom, offs, out):
             if by_slot is None:
                 by_slot = ring.tile([P, PACK, N], BF16, name="ds_by_slot")
             for t in places:
-                bank = psum.tile([P, N], F32, name="dp_bank", tag="work", bufs=7)
+                bank = psum.tile([P, N], F32, name="dp_bank", tag="dp_out", bufs=3)
                 matmul(bank[:], left_mx["do", g], E5M2, slice(t * P, (t + 1) * P), c_mx, E4M3, True, True)
                 nc.vector.scalar_tensor_tensor(
                     out=by_slot[:, t, :], in0=bank[:], scalar=gates[:, g, t : t + 1], in1=weights[g][:, t, :], op0=MULT, op1=MULT
@@ -196,7 +196,7 @@ def tile_attend_gat_exp_c_kernel(tc, qT, cT, doT, rw, qm, dom, offs, out):
         def interleave_grads(bf, by_slot, engine, slots):
             copy_on(
                 engine,
-                bf.rearrange("p (c i) t -> p c t i", i=4),
+                bf[:, slots, :].rearrange("p (c i) t -> p c t i", i=4),
                 by_slot[:, :, slots].rearrange("p t (c i) -> p c t i", i=4),
             )
 
@@ -205,8 +205,9 @@ def tile_attend_gat_exp_c_kernel(tc, qT, cT, doT, rw, qm, dom, offs, out):
             quantize(mx, fmt, bf[:].rearrange("p i t -> p (i t)"))
             moving[name, g] = mx
 
-        def right_cast(name, dt, engine, tag=""):
-            bf = keep.tile([P, GROUPS, P, PACK], BF16, name="%s_bf%d" % (name, dt), align_bytes=64, tag=tag)
+        def right_cast(name, dt, engine, tag="", bf=None):
+            if bf is None:
+                bf = keep.tile([P, GROUPS, P, PACK], BF16, name="%s_bf%d" % (name, dt), align_bytes=64, tag=tag)
             copy_on(
                 engine,
                 bf[:].rearrange("p g (c i) j -> p g c j i", i=4),
@@ -220,7 +221,7 @@ def tile_attend_gat_exp_c_kernel(tc, qT, cT, doT, rw, qm, dom, offs, out):
             return mx
 
         def output_tile(dt, dom_mx, qm_mx):
-            bank = psum.tile([P, N], F32, name="out_bank", tag="work", bufs=7)
+            bank = psum.tile([P, N], F32, name="out_bank", tag="dp_out", bufs=3)
             first, second = slice(0, P), slice(P, 2 * P)
             passes = [
                 (qm_mx, E4M3, first, moving["ds", 0], E5M2),
@@ -251,28 +252,26 @@ def tile_attend_gat_exp_c_kernel(tc, qT, cT, doT, rw, qm, dom, offs, out):
         left_cast("q", 1, 1, "S")
         left_quantize("q", 1, E4M3)
         left_cast("do", 1, 0, "S")
-        ds0b = keep.tile([P, HALF, PACK], BF16, name="ds0b_bf", align_bytes=64)
-        interleave_grads(ds0b[:], ds0, "S", slice(HALF, N))
         scores(1)
         left_cast("do", 1, 1, "V")
         left_quantize("do", 1, E5M2)
-        ds0a = keep.tile([P, HALF, PACK], BF16, name="ds0a_bf", align_bytes=64, tag="left_q1")
-        interleave_grads(ds0a[:], ds0, "V", slice(0, HALF))
+        ds0_bf = keep.tile([P, N, PACK], BF16, name="ds0_bf", align_bytes=64, tag="left_q1")
+        interleave_grads(ds0_bf, ds0, "V", slice(0, 256))
         quantize_half("pw", 0, E4M3, 0, pw0a, "left_do1")
         ds1 = score_grads(1)
         pw0b = keep.tile([P, HALF, PACK], BF16, name="pw0b_bf", align_bytes=64, tag="left_do0")
         gated_on_gpsimd(0, pw0b[:], slice(HALF, N))
+        interleave_grads(ds0_bf, ds0, "S", slice(256, N))
         dom0 = right_cast("dom", 0, "S")
         qm0 = right_cast("qm", 0, "S")
         ds1_bf = keep.tile([P, N, PACK], BF16, name="ds1_bf", align_bytes=64)
-        interleave_grads(ds1_bf[:, :HALF], ds1, "S", slice(0, HALF))
-        interleave_grads(ds1_bf[:, HALF:], ds1, "S", slice(HALF, N))
+        interleave_grads(ds1_bf, ds1, "S", slice(0, HALF))
+        interleave_grads(ds1_bf, ds1, "S", slice(HALF, N))
         pw1 = keep.tile([P, N, PACK], BF16, name="pw1_bf", align_bytes=64, tag="do1_codes")
         gated_on_gpsimd(1, pw1[:, :128], slice(0, 128))
         gated_on_vector(1, pw1[:, 128:], slice(128, N))
         qm0 = right_quantize("qm", 0, E4M3, qm0, "p32_0")
-        quantize_half("ds", 0, E5M2, 0, ds0a, "c_codes")
-        quantize_half("ds", 0, E5M2, 1, ds0b)
+        quantize_moving("ds", 0, E5M2, ds0_bf, "c_codes")
         dom0 = right_quantize("dom", 0, E5M2, dom0, "")
         quantize_half("pw", 0, E4M3, 1, pw0b)
         quantize_moving("pw", 1, E4M3, pw1)
@@ -284,8 +283,9 @@ def tile_attend_gat_exp_c_kernel(tc, qT, cT, doT, rw, qm, dom, offs, out):
         dom2 = right_cast("dom", 2, "S", "")
         output_tile(0, dom0, qm0)
         dom2 = right_quantize("dom", 2, E5M2, dom2)
-        qm2 = right_cast("qm", 2, "S", "p32_0")
-        dom3 = right_cast("dom", 3, "S", "dom_t0_codes")
+        late = keep.tile([P, 2, GROUPS, P, PACK], BF16, name="late_bf", align_bytes=64, tag="p32_0")
+        qm2 = right_cast("qm", 2, "S", bf=late[:, 0])
+        dom3 = right_cast("dom", 3, "S", bf=late[:, 1])
         qm2 = right_quantize("qm", 2, E4M3, qm2)
         dom3 = right_quantize("dom", 3, E5M2, dom3)
         output_tile(1, dom1, qm1)

@@ -43,8 +43,9 @@ def tile_attend_gat_exp_c_kernel(tc, qT, cT, doT, rw, qm, dom, offs, out):
         ring = ctx.enter_context(tc.tile_pool(name="ring", bufs=2))
         psum = ctx.enter_context(tc.psum_pool(name="psum", bufs=1))
 
-        def mx_tiles(name, width, tag=""):
-            codes = keep.tile([P, width], U32, name=name + "_codes", align_bytes=64, tag=tag)
+        def mx_tiles(name, width, codes=None):
+            if codes is None:
+                codes = keep.tile([P, width], U32, name=name + "_codes", align_bytes=64)
             scales = keep.tile([P, width], U8, name=name + "_scales", align_bytes=64)
             return codes, scales
 
@@ -67,12 +68,12 @@ def tile_attend_gat_exp_c_kernel(tc, qT, cT, doT, rw, qm, dom, offs, out):
         nc.sync.dma_start(offsets[:], offs)
         padded = keep.tile([P, P], F32, name="padded")
         nc.vector.memset(padded[:], 0.0)
-        gates = keep.tile([P, GROUPS, PACK], F32, name="gates")
+        gates = keep.tile([P, GROUPS, PACK], F32, name="gates", align_bytes=64)
         nc.scalar.dma_start(out=gates[:], in_=rw[0].rearrange("(g p t) o -> p g (t o)", g=GROUPS, t=PACK))
         nc.vector.tensor_copy(out=padded[:, : GROUPS * PACK], in_=gates[:].rearrange("p g t -> p (g t)"))
         identity = keep.tile([P, P], F32, name="identity")
         make_identity(nc, identity[:])
-        turned_bank = psum.tile([P, P], F32, name="out_bank", tag="dp_out", bufs=3)
+        turned_bank = psum.tile([P, P], F32, name="out_bank", tag="work", bufs=7)
         nc.tensor.transpose(turned_bank[:], padded[:], identity[:])
         turned = keep.tile([P, P], F32, name="turned")
         nc.scalar.copy(out=turned[:], in_=turned_bank[:])
@@ -92,7 +93,7 @@ def tile_attend_gat_exp_c_kernel(tc, qT, cT, doT, rw, qm, dom, offs, out):
             for name, src in (("q", qT), ("do", doT)):
                 rows = src[0].rearrange("(p j) r -> p j r", j=PACK)
                 for h in range(2):
-                    raw = keep.tile([P, PACK, HALF], F32, name="%s_raw%d%d" % (name, g, h))
+                    raw = keep.tile([P, PACK, HALF], F32, name="%s_raw%d%d" % (name, g, h), align_bytes=64)
                     r0 = g * K_PASS + h * HALF
                     nc.sync.dma_start(out=raw[:], in_=rows[:, :, r0 : r0 + HALF])
                     left_raw[name, g, h] = raw
@@ -153,7 +154,7 @@ def tile_attend_gat_exp_c_kernel(tc, qT, cT, doT, rw, qm, dom, offs, out):
             if g not in weights:
                 weights[g] = keep.tile([P, PACK, N], F32, name="p32_%d" % g, align_bytes=64)
             for t in places:
-                bank = psum.tile([P, N], F32, name="a_bank", bufs=4)
+                bank = psum.tile([P, N], F32, name="a_bank", tag="work", bufs=7)
                 matmul(bank[:], left_mx["q", g], E4M3, slice(t * P, (t + 1) * P), c_mx, E4M3, True, True)
                 nc.scalar.activation(out=weights[g][:, t, :], in_=bank[:], func=EXP)
 
@@ -177,16 +178,11 @@ def tile_attend_gat_exp_c_kernel(tc, qT, cT, doT, rw, qm, dom, offs, out):
                 op=MULT,
             )
 
-        def quantize_half(name, g, fmt, h, bf, tag=""):
-            if h == 0:
-                moving[name, g] = mx_tiles("%s%d" % (name, g), N, tag)
-            quantize(moving[name, g], fmt, bf[:].rearrange("p i t -> p (i t)"), slice(h * HALF, (h + 1) * HALF))
-
         def score_grads(g, places=range(PACK), by_slot=None):
             if by_slot is None:
                 by_slot = ring.tile([P, PACK, N], BF16, name="ds_by_slot")
             for t in places:
-                bank = psum.tile([P, N], F32, name="dp_bank", tag="dp_out", bufs=3)
+                bank = psum.tile([P, N], F32, name="dp_bank", tag="work", bufs=7)
                 matmul(bank[:], left_mx["do", g], E5M2, slice(t * P, (t + 1) * P), c_mx, E4M3, True, True)
                 nc.vector.scalar_tensor_tensor(
                     out=by_slot[:, t, :], in0=bank[:], scalar=gates[:, g, t : t + 1], in1=weights[g][:, t, :], op0=MULT, op1=MULT
@@ -200,8 +196,8 @@ def tile_attend_gat_exp_c_kernel(tc, qT, cT, doT, rw, qm, dom, offs, out):
                 by_slot[:, :, slots].rearrange("p t (c i) -> p c t i", i=4),
             )
 
-        def quantize_moving(name, g, fmt, bf, tag=""):
-            mx = mx_tiles("%s%d" % (name, g), N, tag)
+        def quantize_moving(name, g, fmt, bf, codes=None):
+            mx = mx_tiles("%s%d" % (name, g), N, codes)
             quantize(mx, fmt, bf[:].rearrange("p i t -> p (i t)"))
             moving[name, g] = mx
 
@@ -215,13 +211,13 @@ def tile_attend_gat_exp_c_kernel(tc, qT, cT, doT, rw, qm, dom, offs, out):
             )
             return bf
 
-        def right_quantize(name, dt, fmt, bf, tag=""):
-            mx = mx_tiles("%s_t%d" % (name, dt), GROUPS * P, tag)
+        def right_quantize(name, dt, fmt, bf, codes=None):
+            mx = mx_tiles("%s_t%d" % (name, dt), GROUPS * P, codes)
             quantize(mx, fmt, bf[:].rearrange("p g d j -> p (g d j)"))
             return mx
 
         def output_tile(dt, dom_mx, qm_mx):
-            bank = psum.tile([P, N], F32, name="out_bank", tag="dp_out", bufs=3)
+            bank = psum.tile([P, N], F32, name="out_bank", tag="work", bufs=7)
             first, second = slice(0, P), slice(P, 2 * P)
             passes = [
                 (qm_mx, E4M3, first, moving["ds", 0], E5M2),
@@ -246,44 +242,47 @@ def tile_attend_gat_exp_c_kernel(tc, qT, cT, doT, rw, qm, dom, offs, out):
         left_cast("do", 0, 1, "V")
         left_quantize("do", 0, E5M2)
         ds0 = score_grads(0)
-        pw0a = keep.tile([P, HALF, PACK], BF16, name="pw0a_bf", align_bytes=64, tag="left_do0")
-        gated_on_gpsimd(0, pw0a[:], slice(0, HALF))
+        shared = keep.tile([P, 2 * PACK * N - 128 * PACK], BF16, name="shared", align_bytes=64, tag="left_do0")
+        left_bf["do", 1] = shared[:, : PACK * N].rearrange("p (t m j) -> p t m j", t=PACK, j=PACK)
+        pw0 = shared[:, (N - 128) * PACK :].rearrange("p (i t) -> p i t", t=PACK)
+        gated_on_gpsimd(0, pw0[:, HALF:], slice(HALF, N))
         left_cast("q", 1, 0, "S")
         left_cast("q", 1, 1, "S")
         left_quantize("q", 1, E4M3)
         left_cast("do", 1, 0, "S")
         scores(1)
+        ds0_bf = keep.tile([P, N, PACK], BF16, name="ds0_bf", align_bytes=64, tag="q_raw11")
+        interleave_grads(ds0_bf, ds0, "V", slice(0, 384))
         left_cast("do", 1, 1, "V")
         left_quantize("do", 1, E5M2)
-        ds0_bf = keep.tile([P, N, PACK], BF16, name="ds0_bf", align_bytes=64, tag="left_q1")
-        interleave_grads(ds0_bf, ds0, "V", slice(0, 256))
-        quantize_half("pw", 0, E4M3, 0, pw0a, "left_do1")
+        gated_on_vector(0, pw0[:, 128:HALF], slice(128, HALF))
         ds1 = score_grads(1)
-        pw0b = keep.tile([P, HALF, PACK], BF16, name="pw0b_bf", align_bytes=64, tag="left_do0")
-        gated_on_gpsimd(0, pw0b[:], slice(HALF, N))
-        interleave_grads(ds0_bf, ds0, "S", slice(256, N))
+        gated_on_gpsimd(0, pw0[:, :128], slice(0, 128))
+        interleave_grads(ds0_bf, ds0, "S", slice(384, N))
         dom0 = right_cast("dom", 0, "S")
         qm0 = right_cast("qm", 0, "S")
         ds1_bf = keep.tile([P, N, PACK], BF16, name="ds1_bf", align_bytes=64)
         interleave_grads(ds1_bf, ds1, "S", slice(0, HALF))
         interleave_grads(ds1_bf, ds1, "S", slice(HALF, N))
-        pw1 = keep.tile([P, N, PACK], BF16, name="pw1_bf", align_bytes=64, tag="do1_codes")
-        gated_on_gpsimd(1, pw1[:, :128], slice(0, 128))
-        gated_on_vector(1, pw1[:, 128:], slice(128, N))
-        qm0 = right_quantize("qm", 0, E4M3, qm0, "p32_0")
-        quantize_moving("ds", 0, E5M2, ds0_bf, "c_codes")
-        dom0 = right_quantize("dom", 0, E5M2, dom0, "")
-        quantize_half("pw", 0, E4M3, 1, pw0b)
+        pw1 = keep.tile([P, N, PACK], BF16, name="pw1_bf", align_bytes=64)
+        gated_on_gpsimd(1, pw1[:, :224], slice(0, 224))
+        gated_on_vector(1, pw1[:, 224:], slice(224, N))
+        tile0_codes = keep.tile([P, 2 * GROUPS * P], U32, name="tile0_codes", align_bytes=64, tag="gates")
+        group0_codes = keep.tile([P, 2 * N], U32, name="group0_codes", align_bytes=64, tag="p32_1")
+        qm0 = right_quantize("qm", 0, E4M3, qm0, tile0_codes[:, : GROUPS * P])
+        dom0 = right_quantize("dom", 0, E5M2, dom0, tile0_codes[:, GROUPS * P :])
+        quantize_moving("ds", 0, E5M2, ds0_bf, group0_codes[:, :N])
+        quantize_moving("pw", 0, E4M3, pw0, group0_codes[:, N:])
         quantize_moving("pw", 1, E4M3, pw1)
         quantize_moving("ds", 1, E5M2, ds1_bf)
         qm1 = right_cast("qm", 1, "S")
-        dom1 = right_cast("dom", 1, "V", "do1_codes")
         qm1 = right_quantize("qm", 1, E4M3, qm1)
+        dom1 = right_cast("dom", 1, "V", "ds1_bf")
         dom1 = right_quantize("dom", 1, E5M2, dom1)
         dom2 = right_cast("dom", 2, "S", "")
         output_tile(0, dom0, qm0)
         dom2 = right_quantize("dom", 2, E5M2, dom2)
-        late = keep.tile([P, 2, GROUPS, P, PACK], BF16, name="late_bf", align_bytes=64, tag="p32_0")
+        late = keep.tile([P, 2, GROUPS, P, PACK], BF16, name="late_bf", align_bytes=64, tag="gates")
         qm2 = right_cast("qm", 2, "S", bf=late[:, 0])
         dom3 = right_cast("dom", 3, "S", bf=late[:, 1])
         qm2 = right_quantize("qm", 2, E4M3, qm2)

@@ -139,7 +139,7 @@ def tile_attend_gat_exp_c_kernel(tc, qT, cT, doT, rw, qm, dom, offs, out):
                 for lo in (0, 2):
                     copy_on(engine, dst[:, :, :, lo : lo + 2], src[:, :, :, lo : lo + 2])
             else:
-                copy_on(engine, dst, src)
+                copy_on(engine, dst.rearrange("p m j (u e) -> p u m j e", e=2), src.rearrange("p m j (u e) -> p u m j e", e=2))
 
         def left_quantize(name, g, fmt, runs=((0, 1), (1, 2), (2, PACK))):
             bf = left_bf[name, g]
@@ -172,9 +172,9 @@ def tile_attend_gat_exp_c_kernel(tc, qT, cT, doT, rw, qm, dom, offs, out):
         def gated_on_vector(g, bf, slots):
             width = slots.stop - slots.start
             nc.vector.tensor_tensor(
-                out=bf.rearrange("p (c i) t -> p c t i", i=4),
-                in0=weights[g][:, :, slots].rearrange("p t (c i) -> p c t i", i=4),
-                in1=bank_gates[:, g, :].unsqueeze(1).unsqueeze(3).to_broadcast([P, width // 4, PACK, 4]),
+                out=bf.rearrange("p (c i) t -> p c t i", i=2),
+                in0=weights[g][:, :, slots].rearrange("p t (c i) -> p c t i", i=2),
+                in1=bank_gates[:, g, :].unsqueeze(1).unsqueeze(3).to_broadcast([P, width // 2, PACK, 2]),
                 op=MULT,
             )
 
@@ -206,8 +206,8 @@ def tile_attend_gat_exp_c_kernel(tc, qT, cT, doT, rw, qm, dom, offs, out):
                 bf = keep.tile([P, GROUPS, P, PACK], BF16, name="%s_bf%d" % (name, dt), align_bytes=64, tag=tag)
             copy_on(
                 engine,
-                bf[:].rearrange("p g (c i) j -> p g c j i", i=4),
-                right_raw[name, dt].rearrange("p g j (c i) -> p g c j i", i=4),
+                bf[:].rearrange("p g (c i) j -> p g c j i", i=2),
+                right_raw[name, dt].rearrange("p g j (c i) -> p g c j i", i=2),
             )
             return bf
 

@@ -64,8 +64,6 @@ def tile_attend_gat_exp_c_kernel(tc, qT, cT, doT, rw, qm, dom, offs, out):
                 stop=stop,
             )
 
-        offsets = keep.tile([P, N // 16], U16, name="offsets")
-        nc.sync.dma_start(offsets[:], offs)
         padded = keep.tile([P, P], F32, name="padded")
         nc.vector.memset(padded[:], 0.0)
         gates = keep.tile([P, GROUPS, PACK], F32, name="gates", align_bytes=64)
@@ -87,6 +85,9 @@ def tile_attend_gat_exp_c_kernel(tc, qT, cT, doT, rw, qm, dom, offs, out):
             plane = keep.tile([P, T], F32, name="plane%d" % j)
             nc.sync.dma_start(out=plane[:], in_=c_rows[:, j, :])
             planes.append(plane)
+            if j == 0:
+                offsets = keep.tile([P, N // 16], U16, name="offsets")
+                nc.sync.dma_start(offsets[:], offs)
 
         left_raw = {}
         for g in range(GROUPS):
@@ -232,7 +233,12 @@ def tile_attend_gat_exp_c_kernel(tc, qT, cT, doT, rw, qm, dom, offs, out):
             sums = ring.tile([P, N], F32, name="sums")
             nc.scalar.copy(out=sums[:], in_=bank[:])
             nc.vector.tensor_copy(out=windows[dt % WINDOWS][:].indirect(offsets[:]), in_=sums[:])
-            nc.sync.dma_start(out=out[dt * P : (dt + 1) * P, :], in_=windows[dt % WINDOWS][:])
+            window = windows[dt % WINDOWS]
+            if dt < D_TILES - 1:
+                nc.sync.dma_start(out=out[dt * P : (dt + 1) * P, :], in_=window[:])
+            else:
+                nc.sync.dma_start(out=out[dt * P : (dt + 1) * P, : T // 2], in_=window[:, : T // 2])
+                nc.scalar.dma_start(out=out[dt * P : (dt + 1) * P, T // 2 :], in_=window[:, T // 2 :])
 
         left_cast("q", 0, 0, "S")
         left_cast("q", 0, 1, "V")

@@ -25,6 +25,8 @@ D_TILES = D // P
 HALF = K_PASS // 2
 WINDOWS = 3
 M_LOADS = ((0, 1), (1, 2), (2, 4))
+PAIRS = ((0, 2), (2, PACK))
+LATE0, G1, EARLY, TAIL = 128, 200, 128, 128
 
 
 def tile_attend_gat_exp_c_kernel(tc, qT, cT, doT, rw, qm, dom, offs, out):
@@ -65,10 +67,10 @@ def tile_attend_gat_exp_c_kernel(tc, qT, cT, doT, rw, qm, dom, offs, out):
             )
 
         padded = keep.tile([P, P], F32, name="padded")
-        nc.vector.memset(padded[:], 0.0)
+        nc.gpsimd.memset(padded[:], 0.0)
         gates = keep.tile([P, GROUPS, PACK], F32, name="gates", align_bytes=64)
         nc.scalar.dma_start(out=gates[:], in_=rw[0].rearrange("(g p t) o -> p g (t o)", g=GROUPS, t=PACK))
-        nc.vector.tensor_copy(out=padded[:, : GROUPS * PACK], in_=gates[:].rearrange("p g t -> p (g t)"))
+        nc.scalar.copy(out=padded[:, : GROUPS * PACK], in_=gates[:].rearrange("p g t -> p (g t)"))
         identity = keep.tile([P, P], F32, name="identity")
         make_identity(nc, identity[:])
         turned_bank = psum.tile([P, P], F32, name="out_bank", tag="work", bufs=7)
@@ -102,7 +104,7 @@ def tile_attend_gat_exp_c_kernel(tc, qT, cT, doT, rw, qm, dom, offs, out):
         right_raw = {}
         for lo, hi in M_LOADS:
             for name, src in (("dom", dom), ("qm", qm)):
-                raw = keep.tile([P, GROUPS, PACK, (hi - lo) * P], F32, name="%s_raw%d" % (name, lo))
+                raw = keep.tile([P, GROUPS, PACK, (hi - lo) * P], F32, name="%s_raw%d" % (name, lo), align_bytes=64)
                 for g in range(GROUPS):
                     rows = src[0, g * K_PASS : (g + 1) * K_PASS, :].rearrange("(p j) d -> p j d", j=PACK)
                     nc.sync.dma_start(out=raw[:, g], in_=rows[:, :, lo * P : hi * P])
@@ -130,13 +132,13 @@ def tile_attend_gat_exp_c_kernel(tc, qT, cT, doT, rw, qm, dom, offs, out):
 
         left_bf = {}
 
-        def left_cast(name, g, h, engine, tag=""):
+        def left_cast(name, g, h, engine, tag="", cut=False):
             if (name, g) not in left_bf:
                 left_bf[name, g] = keep.tile([P, PACK, P, PACK], BF16, name="left_bf", align_bytes=64, tag=tag or "left_%s%d" % (name, g))
             m = slice(h * (P // 2), (h + 1) * (P // 2))
             dst = left_bf[name, g][:, :, m, :].rearrange("p t m j -> p m j t")
             src = left_raw[name, g, h][:].rearrange("p j (m t) -> p m j t", t=PACK)
-            if engine == "V" and h == 1:
+            if cut:
                 for lo in (0, 2):
                     copy_on(engine, dst[:, :, :, lo : lo + 2], src[:, :, :, lo : lo + 2])
             else:
@@ -179,7 +181,7 @@ def tile_attend_gat_exp_c_kernel(tc, qT, cT, doT, rw, qm, dom, offs, out):
                 op=MULT,
             )
 
-        def score_grads(g, places=range(PACK), by_slot=None):
+        def score_grads(g, places=range(PACK), by_slot=None, warm=()):
             if by_slot is None:
                 by_slot = ring.tile([P, PACK, N], BF16, name="ds_by_slot")
             for t in places:
@@ -188,6 +190,8 @@ def tile_attend_gat_exp_c_kernel(tc, qT, cT, doT, rw, qm, dom, offs, out):
                 nc.vector.scalar_tensor_tensor(
                     out=by_slot[:, t, :], in0=bank[:], scalar=gates[:, g, t : t + 1], in1=weights[g][:, t, :], op0=MULT, op1=MULT
                 )
+                if t in warm:
+                    matmul(bank[:], left_mx["do", g], E5M2, slice(t * P, (t + 1) * P), c_mx, E4M3, True, True)
             return by_slot
 
         def interleave_grads(bf, by_slot, engine, slots):
@@ -217,6 +221,12 @@ def tile_attend_gat_exp_c_kernel(tc, qT, cT, doT, rw, qm, dom, offs, out):
             quantize(mx, fmt, bf[:].rearrange("p g d j -> p (g d j)"))
             return mx
 
+        def quantize_tiles(name, fmt, bf, count):
+            codes, scales = mx_tiles(name, count * GROUPS * P)
+            quantize((codes, scales), fmt, bf.rearrange("p n g d j -> p (n g d j)"))
+            width = GROUPS * P
+            return [(codes[:, n * width : (n + 1) * width], scales[:, n * width : (n + 1) * width]) for n in range(count)]
+
         def output_tile(dt, dom_mx, qm_mx):
             bank = psum.tile([P, N], F32, name="out_bank", tag="work", bufs=7)
             first, second = slice(0, P), slice(P, 2 * P)
@@ -226,8 +236,10 @@ def tile_attend_gat_exp_c_kernel(tc, qT, cT, doT, rw, qm, dom, offs, out):
                 (dom_mx, E5M2, second, moving["pw", 1], E4M3),
                 (qm_mx, E4M3, second, moving["ds", 1], E5M2),
             ]
-            if dt >= 2:
+            if 0 < dt < D_TILES - 1:
                 passes = passes[1:3] + passes[:1] + passes[3:]
+            elif dt > 0:
+                passes = passes[:1] + passes[3:] + passes[1:3]
             for n, operands in enumerate(passes):
                 matmul(bank[:], *operands, n == 0, n == len(passes) - 1)
             sums = ring.tile([P, N], F32, name="sums")
@@ -241,60 +253,66 @@ def tile_attend_gat_exp_c_kernel(tc, qT, cT, doT, rw, qm, dom, offs, out):
                 nc.scalar.dma_start(out=out[dt * P : (dt + 1) * P, T // 2 :], in_=window[:, T // 2 :])
 
         left_cast("q", 0, 0, "S")
-        left_cast("q", 0, 1, "V")
+        left_cast("q", 0, 1, "V", cut=True)
         left_quantize("q", 0, E4M3)
         scores(0)
         left_cast("do", 0, 0, "V")
-        left_cast("do", 0, 1, "V")
+        left_cast("do", 0, 1, "V", cut=True)
         left_quantize("do", 0, E5M2)
-        ds0 = score_grads(0)
-        shared = keep.tile([P, 2 * PACK * N - 128 * PACK], BF16, name="shared", align_bytes=64, tag="left_do0")
-        left_bf["do", 1] = shared[:, : PACK * N].rearrange("p (t m j) -> p t m j", t=PACK, j=PACK)
-        pw0 = shared[:, (N - 128) * PACK :].rearrange("p (i t) -> p i t", t=PACK)
+        ds0 = keep.tile([P, PACK, N], BF16, name="ds0", align_bytes=64)
+        score_grads(0, by_slot=ds0, warm=(0, 1, 2, 3))
+        shared = keep.tile([P, 3 * N - LATE0, PACK], BF16, name="shared", align_bytes=64, tag="left_do0")
+        left_bf["do", 1] = shared[:, :N].rearrange("p (t m) j -> p t m j", t=PACK)
+        pw0, pw1 = shared[:, N - LATE0 : 2 * N - LATE0], shared[:, 2 * N - LATE0 :]
         gated_on_gpsimd(0, pw0[:, HALF:], slice(HALF, N))
+        gated_on_vector(0, pw0[:, LATE0:HALF], slice(LATE0, HALF))
         left_cast("q", 1, 0, "S")
         left_cast("q", 1, 1, "S")
-        left_quantize("q", 1, E4M3)
         left_cast("do", 1, 0, "S")
-        scores(1)
-        ds0_bf = keep.tile([P, N, PACK], BF16, name="ds0_bf", align_bytes=64, tag="q_raw11")
-        interleave_grads(ds0_bf, ds0, "V", slice(0, 384))
+        left_quantize("q", 1, E4M3, PAIRS[:1])
         left_cast("do", 1, 1, "V")
-        left_quantize("do", 1, E5M2)
-        gated_on_vector(0, pw0[:, 128:HALF], slice(128, HALF))
-        ds1 = score_grads(1)
-        gated_on_gpsimd(0, pw0[:, :128], slice(0, 128))
-        interleave_grads(ds0_bf, ds0, "S", slice(384, N))
-        dom0 = right_cast("dom", 0, "S")
+        left_quantize("q", 1, E4M3, PAIRS[1:])
+        ds0_bf = keep.tile([P, N, PACK], BF16, name="ds0_bf", align_bytes=64, tag="do_raw10")
+        interleave_grads(ds0_bf, ds0, "S", slice(0, EARLY))
+        scores(1)
+        left_quantize("do", 1, E5M2, PAIRS[:1])
+        dom0 = right_cast("dom", 0, "V")
+        left_quantize("do", 1, E5M2, PAIRS[1:])
+        ds1 = keep.tile([P, PACK, N], BF16, name="ds1", align_bytes=64, tag="dom_raw0")
+        score_grads(1, by_slot=ds1)
+        gated_on_gpsimd(0, pw0[:, :LATE0], slice(0, LATE0))
         qm0 = right_cast("qm", 0, "S")
+        interleave_grads(ds0_bf, ds0, "S", slice(EARLY, N))
         ds1_bf = keep.tile([P, N, PACK], BF16, name="ds1_bf", align_bytes=64)
-        interleave_grads(ds1_bf, ds1, "S", slice(0, HALF))
-        interleave_grads(ds1_bf, ds1, "S", slice(HALF, N))
-        pw1 = keep.tile([P, N, PACK], BF16, name="pw1_bf", align_bytes=64)
-        gated_on_gpsimd(1, pw1[:, :224], slice(0, 224))
-        gated_on_vector(1, pw1[:, 224:], slice(224, N))
+        interleave_grads(ds1_bf, ds1, "S", slice(0, N - TAIL))
+        gated_on_gpsimd(1, pw1[:, :G1], slice(0, G1))
+        gated_on_vector(1, pw1[:, G1:], slice(G1, N))
+        interleave_grads(ds1_bf, ds1, "V", slice(N - TAIL, N))
         tile0_codes = keep.tile([P, 2 * GROUPS * P], U32, name="tile0_codes", align_bytes=64, tag="gates")
         group0_codes = keep.tile([P, 2 * N], U32, name="group0_codes", align_bytes=64, tag="p32_1")
         qm0 = right_quantize("qm", 0, E4M3, qm0, tile0_codes[:, : GROUPS * P])
         dom0 = right_quantize("dom", 0, E5M2, dom0, tile0_codes[:, GROUPS * P :])
+        warm_bank = psum.tile([P, N], F32, name="warm_bank", tag="work", bufs=7)
+        matmul(warm_bank[:], qm0, E4M3, slice(0, P), c_mx, E4M3, True, True)
+        warm_bank = psum.tile([P, N], F32, name="warm_bank", tag="work", bufs=7)
+        matmul(warm_bank[:], dom0, E5M2, slice(0, P), c_mx, E4M3, True, True)
         quantize_moving("ds", 0, E5M2, ds0_bf, group0_codes[:, :N])
         quantize_moving("pw", 0, E4M3, pw0, group0_codes[:, N:])
         quantize_moving("pw", 1, E4M3, pw1)
         quantize_moving("ds", 1, E5M2, ds1_bf)
         qm1 = right_cast("qm", 1, "S")
+        dom12 = keep.tile([P, 2, GROUPS, P, PACK], BF16, name="dom12", align_bytes=64, tag="do_raw10")
+        right_cast("dom", 1, "V", bf=dom12[:, 0])
         qm1 = right_quantize("qm", 1, E4M3, qm1)
-        dom1 = right_cast("dom", 1, "V", "ds1_bf")
-        dom1 = right_quantize("dom", 1, E5M2, dom1)
-        dom2 = right_cast("dom", 2, "S", "")
+        right_cast("dom", 2, "S", bf=dom12[:, 1])
+        dom1, dom2 = quantize_tiles("dom12", E5M2, dom12[:], 2)
         output_tile(0, dom0, qm0)
-        dom2 = right_quantize("dom", 2, E5M2, dom2)
         late = keep.tile([P, 2, GROUPS, P, PACK], BF16, name="late_bf", align_bytes=64, tag="gates")
-        qm2 = right_cast("qm", 2, "S", bf=late[:, 0])
-        dom3 = right_cast("dom", 3, "S", bf=late[:, 1])
-        qm2 = right_quantize("qm", 2, E4M3, qm2)
-        dom3 = right_quantize("dom", 3, E5M2, dom3)
+        right_cast("qm", 2, "S", bf=late[:, 0])
+        right_cast("qm", 3, "S", bf=late[:, 1])
+        qm2, qm3 = quantize_tiles("qm23", E4M3, late[:], 2)
         output_tile(1, dom1, qm1)
-        qm3 = right_cast("qm", 3, "S", "qm_t1_codes")
-        qm3 = right_quantize("qm", 3, E4M3, qm3)
+        dom3 = right_cast("dom", 3, "S", "qm_t1_codes")
+        dom3 = right_quantize("dom", 3, E5M2, dom3)
         output_tile(2, dom2, qm2)
         output_tile(3, dom3, qm3)

@@ -26,7 +26,7 @@ HALF = K_PASS // 2
 WINDOWS = 3
 M_LOADS = ((0, 1), (1, 2), (2, 4))
 PAIRS = ((0, 2), (2, PACK))
-LATE0, G1, EARLY, TAIL = 128, 200, 128, 128
+LATE0, G1, EARLY = 128, 240, 128
 
 
 def tile_attend_gat_exp_c_kernel(tc, qT, cT, doT, rw, qm, dom, offs, out):
@@ -246,11 +246,9 @@ def tile_attend_gat_exp_c_kernel(tc, qT, cT, doT, rw, qm, dom, offs, out):
             nc.scalar.copy(out=sums[:], in_=bank[:])
             nc.vector.tensor_copy(out=windows[dt % WINDOWS][:].indirect(offsets[:]), in_=sums[:])
             window = windows[dt % WINDOWS]
-            if dt < D_TILES - 1:
-                nc.sync.dma_start(out=out[dt * P : (dt + 1) * P, :], in_=window[:])
-            else:
-                nc.sync.dma_start(out=out[dt * P : (dt + 1) * P, : T // 2], in_=window[:, : T // 2])
-                nc.scalar.dma_start(out=out[dt * P : (dt + 1) * P, T // 2 :], in_=window[:, T // 2 :])
+            second_queue = nc.scalar if dt == D_TILES - 1 else nc.sync
+            nc.sync.dma_start(out=out[dt * P : (dt + 1) * P, : T // 2], in_=window[:, : T // 2])
+            second_queue.dma_start(out=out[dt * P : (dt + 1) * P, T // 2 :], in_=window[:, T // 2 :])
 
         left_cast("q", 0, 0, "S")
         left_cast("q", 0, 1, "V", cut=True)
@@ -284,10 +282,9 @@ def tile_attend_gat_exp_c_kernel(tc, qT, cT, doT, rw, qm, dom, offs, out):
         qm0 = right_cast("qm", 0, "S")
         interleave_grads(ds0_bf, ds0, "S", slice(EARLY, N))
         ds1_bf = keep.tile([P, N, PACK], BF16, name="ds1_bf", align_bytes=64)
-        interleave_grads(ds1_bf, ds1, "S", slice(0, N - TAIL))
+        interleave_grads(ds1_bf, ds1, "S", slice(0, N))
         gated_on_gpsimd(1, pw1[:, :G1], slice(0, G1))
         gated_on_vector(1, pw1[:, G1:], slice(G1, N))
-        interleave_grads(ds1_bf, ds1, "V", slice(N - TAIL, N))
         tile0_codes = keep.tile([P, 2 * GROUPS * P], U32, name="tile0_codes", align_bytes=64, tag="gates")
         group0_codes = keep.tile([P, 2 * N], U32, name="group0_codes", align_bytes=64, tag="p32_1")
         qm0 = right_quantize("qm", 0, E4M3, qm0, tile0_codes[:, : GROUPS * P])

@@ -66,20 +66,8 @@ def tile_attend_gat_exp_c_kernel(tc, qT, cT, doT, rw, qm, dom, offs, out):
                 stop=stop,
             )
 
-        padded = keep.tile([P, P], F32, name="padded")
-        nc.gpsimd.memset(padded[:], 0.0)
-        gates = keep.tile([P, GROUPS, PACK], F32, name="gates", align_bytes=64)
-        nc.scalar.dma_start(out=gates[:], in_=rw[0].rearrange("(g p t) o -> p g (t o)", g=GROUPS, t=PACK))
-        nc.scalar.copy(out=padded[:, : GROUPS * PACK], in_=gates[:].rearrange("p g t -> p (g t)"))
-        identity = keep.tile([P, P], F32, name="identity")
-        make_identity(nc, identity[:])
-        turned_bank = psum.tile([P, P], F32, name="out_bank", tag="work", bufs=7)
-        nc.tensor.transpose(turned_bank[:], padded[:], identity[:])
-        turned = keep.tile([P, P], F32, name="turned")
-        nc.scalar.copy(out=turned[:], in_=turned_bank[:])
-        gate_bank = psum.tile([P, P], F32, name="gate_bank")
-        nc.tensor.transpose(gate_bank[:], turned[:], identity[:])
-        bank_gates = gate_bank[:, : GROUPS * PACK].rearrange("p (g t) -> p g t", t=PACK)
+        gate_rows = keep.tile([P, K_PASS], F32, name="gate_rows")
+        nc.gpsimd.memset(gate_rows[:], 0.0)
 
         c_rows = cT.rearrange("(p j) x -> p j x", j=PACK)
         planes = []
@@ -90,6 +78,16 @@ def tile_attend_gat_exp_c_kernel(tc, qT, cT, doT, rw, qm, dom, offs, out):
             if j == 0:
                 offsets = keep.tile([P, N // 16], U16, name="offsets")
                 nc.sync.dma_start(offsets[:], offs)
+                nc.sync.dma_start(out=gate_rows[:GROUPS, :], in_=rw[0].rearrange("(g r) o -> g (r o)", g=GROUPS))
+
+        identity = keep.tile([P, P], F32, name="identity")
+        make_identity(nc, identity[:])
+        gate_bank = psum.tile([P, PACK, P], F32, name="gate_bank")
+        for t in range(PACK):
+            nc.tensor.transpose(gate_bank[:, t], gate_rows[:, t::PACK], identity[:])
+        bank_gates = gate_bank[:, :, :GROUPS].rearrange("p t g -> p g t")
+        gates = keep.tile([P, GROUPS, PACK], F32, name="gates", align_bytes=64)
+        nc.scalar.copy(out=gates[:], in_=bank_gates)
 
         left_raw = {}
         for g in range(GROUPS):

@@ -272,13 +272,14 @@ def tile_attend_gat_exp_c_kernel(tc, qT, cT, doT, rw, qm, dom, offs, out):
         interleave_grads(ds0_bf, ds0, "S", slice(0, EARLY))
         scores(1)
         left_quantize("do", 1, E5M2, PAIRS[:1])
-        dom0 = right_cast("dom", 0, "V")
+        interleave_grads(ds0_bf, ds0, "V", slice(EARLY, EARLY + HALF))
         left_quantize("do", 1, E5M2, PAIRS[1:])
-        ds1 = keep.tile([P, PACK, N], BF16, name="ds1", align_bytes=64, tag="dom_raw0")
+        ds1 = keep.tile([P, PACK, N], BF16, name="ds1", align_bytes=64, tag="do_raw11")
         score_grads(1, by_slot=ds1)
         gated_on_gpsimd(0, pw0[:, :LATE0], slice(0, LATE0))
+        interleave_grads(ds0_bf, ds0, "S", slice(EARLY + HALF, N))
+        dom0 = right_cast("dom", 0, "S")
         qm0 = right_cast("qm", 0, "S")
-        interleave_grads(ds0_bf, ds0, "S", slice(EARLY, N))
         ds1_bf = keep.tile([P, N, PACK], BF16, name="ds1_bf", align_bytes=64)
         interleave_grads(ds1_bf, ds1, "S", slice(0, N))
         gated_on_gpsimd(1, pw1[:, :G1], slice(0, G1))

@@ -164,9 +164,9 @@ def tile_attend_gat_exp_c_kernel(tc, qT, cT, doT, rw, qm, dom, offs, out):
         def gated_on_gpsimd(g, bf, slots):
             width = slots.stop - slots.start
             nc.gpsimd.tensor_tensor(
-                out=bf,
-                in0=weights[g][:, :, slots].rearrange("p t i -> p i t"),
-                in1=gates[:, g, :].unsqueeze(1).to_broadcast([P, width, PACK]),
+                out=bf.rearrange("p (c i) t -> p c t i", i=4),
+                in0=weights[g][:, :, slots].rearrange("p t (c i) -> p c t i", i=4),
+                in1=gates[:, g, :].unsqueeze(1).unsqueeze(3).to_broadcast([P, width // 4, PACK, 4]),
                 op=MULT,
             )
 

@@ -234,9 +234,9 @@ def tile_attend_gat_exp_c_kernel(tc, qT, cT, doT, rw, qm, dom, offs, out):
                 (dom_mx, E5M2, second, moving["pw", 1], E4M3),
                 (qm_mx, E4M3, second, moving["ds", 1], E5M2),
             ]
-            if 0 < dt < D_TILES - 1:
+            if dt < D_TILES - 1:
                 passes = passes[1:3] + passes[:1] + passes[3:]
-            elif dt > 0:
+            else:
                 passes = passes[:1] + passes[3:] + passes[1:3]
             for n, operands in enumerate(passes):
                 matmul(bank[:], *operands, n == 0, n == len(passes) - 1)
@@ -266,44 +266,44 @@ def tile_attend_gat_exp_c_kernel(tc, qT, cT, doT, rw, qm, dom, offs, out):
         left_cast("q", 1, 1, "S")
         left_cast("do", 1, 0, "S")
         left_quantize("q", 1, E4M3, PAIRS[:1])
-        left_cast("do", 1, 1, "V")
         left_quantize("q", 1, E4M3, PAIRS[1:])
-        ds0_bf = keep.tile([P, N, PACK], BF16, name="ds0_bf", align_bytes=64, tag="do_raw10")
+        ds0_bf = keep.tile([P, N, PACK], BF16, name="ds0_bf", align_bytes=64, tag="q_raw11")
+        interleave_grads(ds0_bf, ds0, "V", slice(EARLY, EARLY + HALF))
+        left_cast("do", 1, 1, "V", cut=True)
         interleave_grads(ds0_bf, ds0, "S", slice(0, EARLY))
         scores(1)
         left_quantize("do", 1, E5M2, PAIRS[:1])
-        interleave_grads(ds0_bf, ds0, "V", slice(EARLY, EARLY + HALF))
         left_quantize("do", 1, E5M2, PAIRS[1:])
         ds1 = keep.tile([P, PACK, N], BF16, name="ds1", align_bytes=64, tag="do_raw11")
         score_grads(1, by_slot=ds1)
         gated_on_gpsimd(0, pw0[:, :LATE0], slice(0, LATE0))
-        interleave_grads(ds0_bf, ds0, "S", slice(EARLY + HALF, N))
         dom0 = right_cast("dom", 0, "S")
         qm0 = right_cast("qm", 0, "S")
+        interleave_grads(ds0_bf, ds0, "S", slice(EARLY + HALF, N))
         ds1_bf = keep.tile([P, N, PACK], BF16, name="ds1_bf", align_bytes=64)
         interleave_grads(ds1_bf, ds1, "S", slice(0, N))
         gated_on_gpsimd(1, pw1[:, :G1], slice(0, G1))
         gated_on_vector(1, pw1[:, G1:], slice(G1, N))
         tile0_codes = keep.tile([P, 2 * GROUPS * P], U32, name="tile0_codes", align_bytes=64, tag="gates")
         group0_codes = keep.tile([P, 2 * N], U32, name="group0_codes", align_bytes=64, tag="p32_1")
-        qm0 = right_quantize("qm", 0, E4M3, qm0, tile0_codes[:, : GROUPS * P])
         dom0 = right_quantize("dom", 0, E5M2, dom0, tile0_codes[:, GROUPS * P :])
-        warm_bank = psum.tile([P, N], F32, name="warm_bank", tag="work", bufs=7)
-        matmul(warm_bank[:], qm0, E4M3, slice(0, P), c_mx, E4M3, True, True)
-        warm_bank = psum.tile([P, N], F32, name="warm_bank", tag="work", bufs=7)
-        matmul(warm_bank[:], dom0, E5M2, slice(0, P), c_mx, E4M3, True, True)
-        quantize_moving("ds", 0, E5M2, ds0_bf, group0_codes[:, :N])
+        for g in range(GROUPS):
+            warm_bank = psum.tile([P, N], F32, name="warm_bank", tag="work", bufs=7)
+            matmul(warm_bank[:], dom0, E5M2, slice(g * P, (g + 1) * P), c_mx, E4M3, True, True)
         quantize_moving("pw", 0, E4M3, pw0, group0_codes[:, N:])
         quantize_moving("pw", 1, E4M3, pw1)
+        qm0 = right_quantize("qm", 0, E4M3, qm0, tile0_codes[:, : GROUPS * P])
+        quantize_moving("ds", 0, E5M2, ds0_bf, group0_codes[:, :N])
         quantize_moving("ds", 1, E5M2, ds1_bf)
-        qm1 = right_cast("qm", 1, "S")
-        dom12 = keep.tile([P, 2, GROUPS, P, PACK], BF16, name="dom12", align_bytes=64, tag="do_raw10")
+        held = keep.tile([P, 3, GROUPS, P, PACK], BF16, name="held", align_bytes=64, tag="do_raw11")
+        qm1 = right_cast("qm", 1, "S", bf=held[:, 2])
+        dom12 = held[:, :2]
         right_cast("dom", 1, "V", bf=dom12[:, 0])
         qm1 = right_quantize("qm", 1, E4M3, qm1)
         right_cast("dom", 2, "S", bf=dom12[:, 1])
-        dom1, dom2 = quantize_tiles("dom12", E5M2, dom12[:], 2)
+        dom1, dom2 = quantize_tiles("dom12", E5M2, dom12, 2)
         output_tile(0, dom0, qm0)
-        late = keep.tile([P, 2, GROUPS, P, PACK], BF16, name="late_bf", align_bytes=64, tag="gates")
+        late = keep.tile([P, 2, GROUPS, P, PACK], BF16, name="late_bf", align_bytes=64, tag="do_raw11")
         right_cast("qm", 2, "S", bf=late[:, 0])
         right_cast("qm", 3, "S", bf=late[:, 1])
         qm2, qm3 = quantize_tiles("qm23", E4M3, late[:], 2)

@@ -26,7 +26,7 @@ HALF = K_PASS // 2
 WINDOWS = 3
 M_LOADS = ((0, 1), (1, 2), (2, 4))
 PAIRS = ((0, 2), (2, PACK))
-LATE0, G1, EARLY = 128, 240, 128
+LATE0, G1, EARLY = 160, 200, 128
 
 
 def tile_attend_gat_exp_c_kernel(tc, qT, cT, doT, rw, qm, dom, offs, out):

@@ -26,7 +26,7 @@ HALF = K_PASS // 2
 WINDOWS = 3
 M_LOADS = ((0, 1), (1, 2), (2, 4))
 PAIRS = ((0, 2), (2, PACK))
-LATE0, G1, EARLY = 160, 200, 128
+LATE0, G1, EARLY, FILL = 160, 200, 128, 176
 
 
 def tile_attend_gat_exp_c_kernel(tc, qT, cT, doT, rw, qm, dom, offs, out):
@@ -268,7 +268,7 @@ def tile_attend_gat_exp_c_kernel(tc, qT, cT, doT, rw, qm, dom, offs, out):
         left_quantize("q", 1, E4M3, PAIRS[:1])
         left_quantize("q", 1, E4M3, PAIRS[1:])
         ds0_bf = keep.tile([P, N, PACK], BF16, name="ds0_bf", align_bytes=64, tag="q_raw11")
-        interleave_grads(ds0_bf, ds0, "V", slice(EARLY, EARLY + HALF))
+        interleave_grads(ds0_bf, ds0, "V", slice(EARLY, EARLY + FILL))
         left_cast("do", 1, 1, "V", cut=True)
         interleave_grads(ds0_bf, ds0, "S", slice(0, EARLY))
         scores(1)
@@ -279,7 +279,7 @@ def tile_attend_gat_exp_c_kernel(tc, qT, cT, doT, rw, qm, dom, offs, out):
         gated_on_gpsimd(0, pw0[:, :LATE0], slice(0, LATE0))
         dom0 = right_cast("dom", 0, "S")
         qm0 = right_cast("qm", 0, "S")
-        interleave_grads(ds0_bf, ds0, "S", slice(EARLY + HALF, N))
+        interleave_grads(ds0_bf, ds0, "S", slice(EARLY + FILL, N))
         ds1_bf = keep.tile([P, N, PACK], BF16, name="ds1_bf", align_bytes=64)
         interleave_grads(ds1_bf, ds1, "S", slice(0, N))
         gated_on_gpsimd(1, pw1[:, :G1], slice(0, G1))

@@ -26,7 +26,7 @@ HALF = K_PASS // 2
 WINDOWS = 3
 M_LOADS = ((0, 1), (1, 2), (2, 4))
 PAIRS = ((0, 2), (2, PACK))
-LATE0, G1, EARLY, FILL = 160, 200, 128, 176
+LATE0, G1, EARLY, FILL = 160, 200, 128, 320
 
 
 def tile_attend_gat_exp_c_kernel(tc, qT, cT, doT, rw, qm, dom, offs, out):

@@ -155,7 +155,7 @@ def tile_attend_gat_exp_c_kernel(tc, qT, cT, doT, rw, qm, dom, offs, out):
             if g not in weights:
                 weights[g] = keep.tile([P, PACK, N], F32, name="p32_%d" % g, align_bytes=64)
             for t in places:
-                bank = psum.tile([P, N], F32, name="a_bank", tag="work", bufs=7)
+                bank = psum.tile([P, N], F32, name="a_bank", tag="work", bufs=5)
                 matmul(bank[:], left_mx["q", g], E4M3, slice(t * P, (t + 1) * P), c_mx, E4M3, True, True)
                 nc.scalar.activation(out=weights[g][:, t, :], in_=bank[:], func=EXP)
 
@@ -183,7 +183,10 @@ def tile_attend_gat_exp_c_kernel(tc, qT, cT, doT, rw, qm, dom, offs, out):
             if by_slot is None:
                 by_slot = ring.tile([P, PACK, N], BF16, name="ds_by_slot")
             for t in places:
-                bank = psum.tile([P, N], F32, name="dp_bank", tag="work", bufs=7)
+                if g == 0 or t < 2:
+                    bank = psum.tile([P, N], F32, name="dp_bank", tag="dp", bufs=2)
+                else:
+                    bank = psum.tile([P, N], F32, name="dp_late_bank", tag="work", bufs=5)
                 matmul(bank[:], left_mx["do", g], E5M2, slice(t * P, (t + 1) * P), c_mx, E4M3, True, True)
                 nc.vector.scalar_tensor_tensor(
                     out=by_slot[:, t, :], in0=bank[:], scalar=gates[:, g, t : t + 1], in1=weights[g][:, t, :], op0=MULT, op1=MULT
@@ -226,7 +229,7 @@ def tile_attend_gat_exp_c_kernel(tc, qT, cT, doT, rw, qm, dom, offs, out):
             return [(codes[:, n * width : (n + 1) * width], scales[:, n * width : (n + 1) * width]) for n in range(count)]
 
         def output_tile(dt, dom_mx, qm_mx):
-            bank = psum.tile([P, N], F32, name="out_bank", tag="work", bufs=7)
+            bank = psum.tile([P, N], F32, name="out_bank", tag="work", bufs=5)
             first, second = slice(0, P), slice(P, 2 * P)
             passes = [
                 (qm_mx, E4M3, first, moving["ds", 0], E5M2),
@@ -248,6 +251,9 @@ def tile_attend_gat_exp_c_kernel(tc, qT, cT, doT, rw, qm, dom, offs, out):
             nc.sync.dma_start(out=out[dt * P : (dt + 1) * P, : T // 2], in_=window[:, : T // 2])
             second_queue.dma_start(out=out[dt * P : (dt + 1) * P, T // 2 :], in_=window[:, T // 2 :])
 
+        for n in range(2):
+            warm_bank = psum.tile([P, N], F32, name="warm_bank", tag="work", bufs=5)
+            matmul(warm_bank[:], c_mx, E4M3, slice(n * P, (n + 1) * P), c_mx, E4M3, True, True)
         left_cast("q", 0, 0, "S")
         left_cast("q", 0, 1, "V", cut=True)
         left_quantize("q", 0, E4M3)
@@ -256,7 +262,7 @@ def tile_attend_gat_exp_c_kernel(tc, qT, cT, doT, rw, qm, dom, offs, out):
         left_cast("do", 0, 1, "V", cut=True)
         left_quantize("do", 0, E5M2)
         ds0 = keep.tile([P, PACK, N], BF16, name="ds0", align_bytes=64)
-        score_grads(0, by_slot=ds0, warm=(0, 1, 2, 3))
+        score_grads(0, by_slot=ds0, warm=())
         shared = keep.tile([P, 3 * N - LATE0, PACK], BF16, name="shared", align_bytes=64, tag="left_do0")
         left_bf["do", 1] = shared[:, :N].rearrange("p (t m) j -> p t m j", t=PACK)
         pw0, pw1 = shared[:, N - LATE0 : 2 * N - LATE0], shared[:, 2 * N - LATE0 :]
@@ -287,9 +293,8 @@ def tile_attend_gat_exp_c_kernel(tc, qT, cT, doT, rw, qm, dom, offs, out):
         tile0_codes = keep.tile([P, 2 * GROUPS * P], U32, name="tile0_codes", align_bytes=64, tag="gates")
         group0_codes = keep.tile([P, 2 * N], U32, name="group0_codes", align_bytes=64, tag="p32_1")
         dom0 = right_quantize("dom", 0, E5M2, dom0, tile0_codes[:, GROUPS * P :])
-        for g in range(GROUPS):
-            warm_bank = psum.tile([P, N], F32, name="warm_bank", tag="work", bufs=7)
-            matmul(warm_bank[:], dom0, E5M2, slice(g * P, (g + 1) * P), c_mx, E4M3, True, True)
+        warm_bank = psum.tile([P, N], F32, name="warm_bank", tag="work", bufs=5)
+        matmul(warm_bank[:], dom0, E5M2, slice(0, P), c_mx, E4M3, True, True)
         quantize_moving("pw", 0, E4M3, pw0, group0_codes[:, N:])
         quantize_moving("pw", 1, E4M3, pw1)
         qm0 = right_quantize("qm", 0, E4M3, qm0, tile0_codes[:, : GROUPS * P])

@@ -26,7 +26,7 @@ HALF = K_PASS // 2
 WINDOWS = 3
 M_LOADS = ((0, 1), (1, 2), (2, 4))
 PAIRS = ((0, 2), (2, PACK))
-LATE0, G1, EARLY, FILL = 160, 200, 128, 320
+LATE0, G1, EARLY, LAST = 128, 232, 64, 128
 
 
 def tile_attend_gat_exp_c_kernel(tc, qT, cT, doT, rw, qm, dom, offs, out):
@@ -261,31 +261,34 @@ def tile_attend_gat_exp_c_kernel(tc, qT, cT, doT, rw, qm, dom, offs, out):
         left_cast("do", 0, 0, "V")
         left_cast("do", 0, 1, "V", cut=True)
         left_quantize("do", 0, E5M2)
-        ds0 = keep.tile([P, PACK, N], BF16, name="ds0", align_bytes=64)
+        pw0_at = PACK * N - LAST
+        group0 = keep.tile([P, pw0_at + PACK * N], BF16, name="group0", align_bytes=64, tag="left_do0")
+        ds0 = group0[:, : PACK * N].rearrange("p (t i) -> p t i", t=PACK)
+        pw0 = group0[:, pw0_at:].rearrange("p (i t) -> p i t", t=PACK)
         score_grads(0, by_slot=ds0, warm=())
-        shared = keep.tile([P, 3 * N - LATE0, PACK], BF16, name="shared", align_bytes=64, tag="left_do0")
-        left_bf["do", 1] = shared[:, :N].rearrange("p (t m) j -> p t m j", t=PACK)
-        pw0, pw1 = shared[:, N - LATE0 : 2 * N - LATE0], shared[:, 2 * N - LATE0 :]
+        pw1 = keep.tile([P, N, PACK], BF16, name="pw1_bf", align_bytes=64)
         gated_on_gpsimd(0, pw0[:, HALF:], slice(HALF, N))
         gated_on_vector(0, pw0[:, LATE0:HALF], slice(LATE0, HALF))
         left_cast("q", 1, 0, "S")
         left_cast("q", 1, 1, "S")
+        shared = keep.tile([P, 2 * N - LAST, PACK], BF16, name="shared", align_bytes=64, tag="q_raw11")
+        ds0_bf = shared[:, :N]
+        left_bf["do", 1] = shared[:, N - LAST :].rearrange("p (t m) j -> p t m j", t=PACK)
         left_cast("do", 1, 0, "S")
         left_quantize("q", 1, E4M3, PAIRS[:1])
         left_quantize("q", 1, E4M3, PAIRS[1:])
-        ds0_bf = keep.tile([P, N, PACK], BF16, name="ds0_bf", align_bytes=64, tag="q_raw11")
-        interleave_grads(ds0_bf, ds0, "V", slice(EARLY, EARLY + FILL))
+        interleave_grads(ds0_bf, ds0, "V", slice(EARLY, N - LAST))
         left_cast("do", 1, 1, "V", cut=True)
         interleave_grads(ds0_bf, ds0, "S", slice(0, EARLY))
         scores(1)
         left_quantize("do", 1, E5M2, PAIRS[:1])
         left_quantize("do", 1, E5M2, PAIRS[1:])
+        interleave_grads(ds0_bf, ds0, "V", slice(N - LAST, N))
         ds1 = keep.tile([P, PACK, N], BF16, name="ds1", align_bytes=64, tag="do_raw11")
         score_grads(1, by_slot=ds1)
         gated_on_gpsimd(0, pw0[:, :LATE0], slice(0, LATE0))
         dom0 = right_cast("dom", 0, "S")
         qm0 = right_cast("qm", 0, "S")
-        interleave_grads(ds0_bf, ds0, "S", slice(EARLY + FILL, N))
         ds1_bf = keep.tile([P, N, PACK], BF16, name="ds1_bf", align_bytes=64)
         interleave_grads(ds1_bf, ds1, "S", slice(0, N))
         gated_on_gpsimd(1, pw1[:, :G1], slice(0, G1))

@@ -130,15 +130,15 @@ def tile_attend_gat_exp_c_kernel(tc, qT, cT, doT, rw, qm, dom, offs, out):
 
         left_bf = {}
 
-        def left_cast(name, g, h, engine, tag="", cut=False):
+        def left_cast(name, g, h, engine, tag="", cut=""):
             if (name, g) not in left_bf:
                 left_bf[name, g] = keep.tile([P, PACK, P, PACK], BF16, name="left_bf", align_bytes=64, tag=tag or "left_%s%d" % (name, g))
             m = slice(h * (P // 2), (h + 1) * (P // 2))
             dst = left_bf[name, g][:, :, m, :].rearrange("p t m j -> p m j t")
             src = left_raw[name, g, h][:].rearrange("p j (m t) -> p m j t", t=PACK)
             if cut:
-                for lo in (0, 2):
-                    copy_on(engine, dst[:, :, :, lo : lo + 2], src[:, :, :, lo : lo + 2])
+                for lo, pair_engine in zip((0, 2), cut):
+                    copy_on(pair_engine, dst[:, :, :, lo : lo + 2], src[:, :, :, lo : lo + 2])
             else:
                 copy_on(engine, dst.rearrange("p m j (u e) -> p u m j e", e=2), src.rearrange("p m j (u e) -> p u m j e", e=2))
 
@@ -255,11 +255,11 @@ def tile_attend_gat_exp_c_kernel(tc, qT, cT, doT, rw, qm, dom, offs, out):
             warm_bank = psum.tile([P, N], F32, name="warm_bank", tag="work", bufs=5)
             matmul(warm_bank[:], c_mx, E4M3, slice(n * P, (n + 1) * P), c_mx, E4M3, True, True)
         left_cast("q", 0, 0, "S")
-        left_cast("q", 0, 1, "V", cut=True)
+        left_cast("q", 0, 1, "V", cut="VS")
         left_quantize("q", 0, E4M3)
         scores(0)
         left_cast("do", 0, 0, "V")
-        left_cast("do", 0, 1, "V", cut=True)
+        left_cast("do", 0, 1, "V", cut="VV")
         left_quantize("do", 0, E5M2)
         pw0_at = PACK * N - LAST
         group0 = keep.tile([P, pw0_at + PACK * N], BF16, name="group0", align_bytes=64, tag="left_do0")
@@ -278,7 +278,7 @@ def tile_attend_gat_exp_c_kernel(tc, qT, cT, doT, rw, qm, dom, offs, out):
         left_quantize("q", 1, E4M3, PAIRS[:1])
         left_quantize("q", 1, E4M3, PAIRS[1:])
         interleave_grads(ds0_bf, ds0, "V", slice(EARLY, N - LAST))
-        left_cast("do", 1, 1, "V", cut=True)
+        left_cast("do", 1, 1, "V", cut="VV")
         interleave_grads(ds0_bf, ds0, "S", slice(0, EARLY))
         scores(1)
         left_quantize("do", 1, E5M2, PAIRS[:1])

@@ -26,7 +26,7 @@ HALF = K_PASS // 2
 WINDOWS = 3
 M_LOADS = ((0, 1), (1, 2), (2, 4))
 PAIRS = ((0, 2), (2, PACK))
-LATE0, G1, EARLY, LAST = 128, 232, 64, 128
+LATE0, G1, EARLY, MIDDLE, LAST, CAST_G = 128, 216, 96, 96, 128, 72
 
 
 def tile_attend_gat_exp_c_kernel(tc, qT, cT, doT, rw, qm, dom, offs, out):
@@ -121,12 +121,17 @@ def tile_attend_gat_exp_c_kernel(tc, qT, cT, doT, rw, qm, dom, offs, out):
         for h in range(2):
             listed = offsets[:, h * HALF // 16 : (h + 1) * HALF // 16]
             nc.vector.tensor_copy(out=c_bf[:, h * HALF : (h + 1) * HALF, PACK - 1], in_=planes[PACK - 1][:].indirect(listed))
-        c_mx = mx_tiles("c", N)
+        def part(mx, start, width):
+            return mx[0][:, start : start + width], mx[1][:, start : start + width]
+
+        pw1_c = mx_tiles("pw1_c", 2 * N)
+        c_mx = part(pw1_c, N, N)
         for h in range(2):
             cols = slice(h * HALF, (h + 1) * HALF)
             quantize(c_mx, E4M3, c_bf[:, cols, :].rearrange("p i j -> p (i j)"), cols)
 
-        left_mx = {}
+        ds1_do = mx_tiles("ds1_do", 2 * N)
+        left_mx = {("do", 1): part(ds1_do, N, K_PASS)}
 
         left_bf = {}
 
@@ -202,11 +207,6 @@ def tile_attend_gat_exp_c_kernel(tc, qT, cT, doT, rw, qm, dom, offs, out):
                 by_slot[:, :, slots].rearrange("p t (c i) -> p c t i", i=4),
             )
 
-        def quantize_moving(name, g, fmt, bf, codes=None):
-            mx = mx_tiles("%s%d" % (name, g), N, codes)
-            quantize(mx, fmt, bf[:].rearrange("p i t -> p (i t)"))
-            moving[name, g] = mx
-
         def right_cast(name, dt, engine, tag="", bf=None):
             if bf is None:
                 bf = keep.tile([P, GROUPS, P, PACK], BF16, name="%s_bf%d" % (name, dt), align_bytes=64, tag=tag)
@@ -222,34 +222,41 @@ def tile_attend_gat_exp_c_kernel(tc, qT, cT, doT, rw, qm, dom, offs, out):
             quantize(mx, fmt, bf[:].rearrange("p g d j -> p (g d j)"))
             return mx
 
-        def quantize_tiles(name, fmt, bf, count):
-            codes, scales = mx_tiles(name, count * GROUPS * P)
-            quantize((codes, scales), fmt, bf.rearrange("p n g d j -> p (n g d j)"))
-            width = GROUPS * P
-            return [(codes[:, n * width : (n + 1) * width], scales[:, n * width : (n + 1) * width]) for n in range(count)]
-
-        def output_tile(dt, dom_mx, qm_mx):
+        def products(passes):
             bank = psum.tile([P, N], F32, name="out_bank", tag="work", bufs=5)
-            first, second = slice(0, P), slice(P, 2 * P)
-            passes = [
-                (qm_mx, E4M3, first, moving["ds", 0], E5M2),
-                (dom_mx, E5M2, first, moving["pw", 0], E4M3),
-                (dom_mx, E5M2, second, moving["pw", 1], E4M3),
-                (qm_mx, E4M3, second, moving["ds", 1], E5M2),
-            ]
-            if dt < D_TILES - 1:
-                passes = passes[1:3] + passes[:1] + passes[3:]
-            else:
-                passes = passes[:1] + passes[3:] + passes[1:3]
             for n, operands in enumerate(passes):
                 matmul(bank[:], *operands, n == 0, n == len(passes) - 1)
-            sums = ring.tile([P, N], F32, name="sums")
-            nc.scalar.copy(out=sums[:], in_=bank[:])
-            nc.vector.tensor_copy(out=windows[dt % WINDOWS][:].indirect(offsets[:]), in_=sums[:])
+            return bank
+
+        def tile_passes(dom_mx, qm_mx, shift=0):
+            passes = []
+            for lhs, lhs_fmt, name, rhs_fmt in ((dom_mx, E5M2, "pw", E4M3), (qm_mx, E4M3, "ds", E5M2)):
+                for g in range(GROUPS):
+                    passes.append((lhs, lhs_fmt, slice(g * P, (g + 1) * P), part(moving[name, g], shift, N), rhs_fmt))
+            return passes
+
+        def copy_sums(bank, width):
+            sums = ring.tile([P, width], F32, name="sums")
+            nc.scalar.copy(out=sums[:], in_=bank[:, :width])
+            return sums
+
+        def scatter(dt, slots, sums):
+            listed = offsets[:, slots.start // 16 : slots.stop // 16]
+            nc.vector.tensor_copy(out=windows[dt % WINDOWS][:].indirect(listed), in_=sums[:])
+
+        def store(dt):
             window = windows[dt % WINDOWS]
             second_queue = nc.scalar if dt == D_TILES - 1 else nc.sync
             nc.sync.dma_start(out=out[dt * P : (dt + 1) * P, : T // 2], in_=window[:, : T // 2])
             second_queue.dma_start(out=out[dt * P : (dt + 1) * P, T // 2 :], in_=window[:, T // 2 :])
+
+        def shared_cast(dt, bf):
+            copy_on("G", bf[:, :, :CAST_G, :], right_raw["qm", dt][:, :, :, :CAST_G].rearrange("p g j d -> p g d j"))
+            copy_on(
+                "S",
+                bf[:, :, CAST_G:, :].rearrange("p g (c i) j -> p g c j i", i=2),
+                right_raw["qm", dt][:, :, :, CAST_G:].rearrange("p g j (c i) -> p g c j i", i=2),
+            )
 
         for n in range(2):
             warm_bank = psum.tile([P, N], F32, name="warm_bank", tag="work", bufs=5)
@@ -277,9 +284,9 @@ def tile_attend_gat_exp_c_kernel(tc, qT, cT, doT, rw, qm, dom, offs, out):
         left_cast("do", 1, 0, "S")
         left_quantize("q", 1, E4M3, PAIRS[:1])
         left_quantize("q", 1, E4M3, PAIRS[1:])
-        interleave_grads(ds0_bf, ds0, "V", slice(EARLY, N - LAST))
+        interleave_grads(ds0_bf, ds0, "V", slice(N - LAST - MIDDLE, N - LAST))
         left_cast("do", 1, 1, "V", cut="VV")
-        interleave_grads(ds0_bf, ds0, "S", slice(0, EARLY))
+        interleave_grads(ds0_bf, ds0, "S", slice(N - LAST - MIDDLE - EARLY, N - LAST - MIDDLE))
         scores(1)
         left_quantize("do", 1, E5M2, PAIRS[:1])
         left_quantize("do", 1, E5M2, PAIRS[1:])
@@ -289,34 +296,65 @@ def tile_attend_gat_exp_c_kernel(tc, qT, cT, doT, rw, qm, dom, offs, out):
         gated_on_gpsimd(0, pw0[:, :LATE0], slice(0, LATE0))
         dom0 = right_cast("dom", 0, "S")
         qm0 = right_cast("qm", 0, "S")
-        ds1_bf = keep.tile([P, N, PACK], BF16, name="ds1_bf", align_bytes=64)
-        interleave_grads(ds1_bf, ds1, "S", slice(0, N))
-        gated_on_gpsimd(1, pw1[:, :G1], slice(0, G1))
-        gated_on_vector(1, pw1[:, G1:], slice(G1, N))
-        tile0_codes = keep.tile([P, 2 * GROUPS * P], U32, name="tile0_codes", align_bytes=64, tag="gates")
-        group0_codes = keep.tile([P, 2 * N], U32, name="group0_codes", align_bytes=64, tag="p32_1")
-        dom0 = right_quantize("dom", 0, E5M2, dom0, tile0_codes[:, GROUPS * P :])
+        first, second = slice(HALF, N), slice(0, HALF)
+        ds1_first = keep.tile([P, HALF, PACK], BF16, name="ds1_first", align_bytes=64)
+        ds1_second = keep.tile([P, HALF, PACK], BF16, name="ds1_second", align_bytes=64)
+        interleave_grads(ds1_first, ds1[:, :, first], "S", slice(0, HALF))
+        interleave_grads(ds0_bf, ds0, "S", slice(0, N - LAST - MIDDLE - EARLY))
+        interleave_grads(ds1_second, ds1[:, :, second], "S", slice(0, HALF))
+        gated_on_gpsimd(1, pw1[:, N - G1 :], slice(N - G1, N))
+        gated_on_vector(1, pw1[:, : N - G1], slice(0, N - G1))
+        wide = N + HALF
+        group0_codes = keep.tile([P, 2 * wide], U32, name="group0_codes", align_bytes=64, tag="gates")
+        pw0_qm = mx_tiles("pw0_qm", wide, group0_codes[:, :wide])
+        ds0_dom = mx_tiles("ds0_dom", wide, group0_codes[:, wide:])
+        moving.update({("pw", 0): pw0_qm, ("pw", 1): pw1_c, ("ds", 0): ds0_dom, ("ds", 1): ds1_do})
+
+        def quantize_half(name, g, bf, slots):
+            quantize(moving[name, g], E4M3 if name == "pw" else E5M2, bf.rearrange("p i t -> p (i t)"), slots)
+
+        quantize(ds0_dom, E5M2, dom0[:].rearrange("p g d j -> p (g d j)"), slice(N, wide))
+        dom0 = part(ds0_dom, N, HALF)
         warm_bank = psum.tile([P, N], F32, name="warm_bank", tag="work", bufs=5)
         matmul(warm_bank[:], dom0, E5M2, slice(0, P), c_mx, E4M3, True, True)
-        quantize_moving("pw", 0, E4M3, pw0, group0_codes[:, N:])
-        quantize_moving("pw", 1, E4M3, pw1)
-        qm0 = right_quantize("qm", 0, E4M3, qm0, tile0_codes[:, : GROUPS * P])
-        quantize_moving("ds", 0, E5M2, ds0_bf, group0_codes[:, :N])
-        quantize_moving("ds", 1, E5M2, ds1_bf)
-        held = keep.tile([P, 3, GROUPS, P, PACK], BF16, name="held", align_bytes=64, tag="do_raw11")
-        qm1 = right_cast("qm", 1, "S", bf=held[:, 2])
-        dom12 = held[:, :2]
-        right_cast("dom", 1, "V", bf=dom12[:, 0])
-        qm1 = right_quantize("qm", 1, E4M3, qm1)
-        right_cast("dom", 2, "S", bf=dom12[:, 1])
-        dom1, dom2 = quantize_tiles("dom12", E5M2, dom12, 2)
-        output_tile(0, dom0, qm0)
-        late = keep.tile([P, 2, GROUPS, P, PACK], BF16, name="late_bf", align_bytes=64, tag="do_raw11")
-        right_cast("qm", 2, "S", bf=late[:, 0])
-        right_cast("qm", 3, "S", bf=late[:, 1])
-        qm2, qm3 = quantize_tiles("qm23", E4M3, late[:], 2)
-        output_tile(1, dom1, qm1)
-        dom3 = right_cast("dom", 3, "S", "qm_t1_codes")
-        dom3 = right_quantize("dom", 3, E5M2, dom3)
-        output_tile(2, dom2, qm2)
-        output_tile(3, dom3, qm3)
+        quantize(pw0_qm, E4M3, qm0[:].rearrange("p g d j -> p (g d j)"), slice(N, wide))
+        qm0 = part(pw0_qm, N, HALF)
+        quantize_half("pw", 0, pw0[:, first], first)
+        quantize_half("pw", 1, pw1[:, first], first)
+        quantize_half("ds", 0, ds0_bf[:, first], first)
+        quantize_half("ds", 1, ds1_first[:], first)
+        first_bank = products(tile_passes(dom0, qm0, HALF))
+        quantize_half("pw", 0, pw0[:, second], second)
+        quantize_half("pw", 1, pw1[:, second], second)
+        quantize_half("ds", 0, ds0_bf[:, second], second)
+        quantize_half("ds", 1, ds1_second[:], second)
+        second_bank = products(tile_passes(dom0, qm0))
+
+        sums = copy_sums(first_bank, HALF)
+        scatter(0, first, sums)
+        later = keep.tile([P, 5, GROUPS, P, PACK], BF16, name="later_bf", align_bytes=64, tag="ds1_second")
+        dom1 = right_cast("dom", 1, "S", bf=later[:, 0])
+        qm1 = later[:, 1]
+        shared_cast(1, qm1)
+        sums = copy_sums(second_bank, HALF)
+        dom1 = right_quantize("dom", 1, E5M2, dom1)
+        qm1_mx = right_quantize("qm", 1, E4M3, qm1)
+        bank = products(tile_passes(dom1, qm1_mx))
+        scatter(0, second, sums)
+        store(0)
+        dom2 = right_cast("dom", 2, "S", bf=later[:, 2])
+        shared_cast(2, qm1)
+        sums = copy_sums(bank, N)
+        dom2 = right_quantize("dom", 2, E5M2, dom2)
+        qm2_mx = right_quantize("qm", 2, E4M3, qm1)
+        bank = products(tile_passes(dom2, qm2_mx))
+        scatter(1, slice(0, N), sums)
+        store(1)
+        dom3 = right_cast("dom", 3, "S", bf=later[:, 3])
+        qm3 = right_cast("qm", 3, "S", bf=later[:, 4])
+        sums = copy_sums(bank, N)
+        bank = products(tile_passes(right_quantize("dom", 3, E5M2, dom3), right_quantize("qm", 3, E4M3, qm3)))
+        scatter(2, slice(0, N), sums)
+        store(2)
+        scatter(3, slice(0, N), copy_sums(bank, N))
+        store(3)

@@ -26,7 +26,7 @@ HALF = K_PASS // 2
 WINDOWS = 3
 M_LOADS = ((0, 1), (1, 2), (2, 4))
 PAIRS = ((0, 2), (2, PACK))
-LATE0, G1, EARLY, MIDDLE, LAST, CAST_G = 128, 216, 96, 96, 128, 72
+LATE0, G1, EARLY, MIDDLE, LAST, CAST_G = 128, 216, 96, 96, 128, 88
 
 
 def tile_attend_gat_exp_c_kernel(tc, qT, cT, doT, rw, qm, dom, offs, out):
@@ -313,17 +313,20 @@ def tile_attend_gat_exp_c_kernel(tc, qT, cT, doT, rw, qm, dom, offs, out):
         def quantize_half(name, g, bf, slots):
             quantize(moving[name, g], E4M3 if name == "pw" else E5M2, bf.rearrange("p i t -> p (i t)"), slots)
 
+        warm_bank = psum.tile([P, N], F32, name="warm_bank", tag="gate_bank")
+        matmul(warm_bank[:], c_mx, E4M3, slice(0, P), c_mx, E4M3, True, True)
         quantize(ds0_dom, E5M2, dom0[:].rearrange("p g d j -> p (g d j)"), slice(N, wide))
         dom0 = part(ds0_dom, N, HALF)
         warm_bank = psum.tile([P, N], F32, name="warm_bank", tag="work", bufs=5)
         matmul(warm_bank[:], dom0, E5M2, slice(0, P), c_mx, E4M3, True, True)
+        quantize_half("pw", 1, pw1[:, first], first)
         quantize(pw0_qm, E4M3, qm0[:].rearrange("p g d j -> p (g d j)"), slice(N, wide))
         qm0 = part(pw0_qm, N, HALF)
         quantize_half("pw", 0, pw0[:, first], first)
-        quantize_half("pw", 1, pw1[:, first], first)
         quantize_half("ds", 0, ds0_bf[:, first], first)
         quantize_half("ds", 1, ds1_first[:], first)
-        first_bank = products(tile_passes(dom0, qm0, HALF))
+        passes = tile_passes(dom0, qm0, HALF)
+        first_bank = products([passes[1], passes[0]] + passes[2:])
         quantize_half("pw", 0, pw0[:, second], second)
         quantize_half("pw", 1, pw1[:, second], second)
         quantize_half("ds", 0, ds0_bf[:, second], second)

@@ -26,7 +26,7 @@ HALF = K_PASS // 2
 WINDOWS = 3
 M_LOADS = ((0, 1), (1, 2), (2, 4))
 PAIRS = ((0, 2), (2, PACK))
-LATE0, G1, EARLY, MIDDLE, LAST, CAST_G = 128, 216, 96, 96, 128, 88
+LATE0, G1, EARLY, MIDDLE, LAST = 128, 216, 96, 96, 128
 
 
 def tile_attend_gat_exp_c_kernel(tc, qT, cT, doT, rw, qm, dom, offs, out):
@@ -251,12 +251,12 @@ def tile_attend_gat_exp_c_kernel(tc, qT, cT, doT, rw, qm, dom, offs, out):
             second_queue.dma_start(out=out[dt * P : (dt + 1) * P, T // 2 :], in_=window[:, T // 2 :])
 
         def shared_cast(dt, bf):
-            copy_on("G", bf[:, :, :CAST_G, :], right_raw["qm", dt][:, :, :, :CAST_G].rearrange("p g j d -> p g d j"))
-            copy_on(
-                "S",
-                bf[:, :, CAST_G:, :].rearrange("p g (c i) j -> p g c j i", i=2),
-                right_raw["qm", dt][:, :, :, CAST_G:].rearrange("p g j (c i) -> p g c j i", i=2),
-            )
+            for g, (engine, run) in enumerate((("S", 2), ("G", 4))):
+                copy_on(
+                    engine,
+                    bf[:, g].rearrange("p (c i) j -> p c j i", i=run),
+                    right_raw["qm", dt][:, g].rearrange("p j (c i) -> p c j i", i=run),
+                )
 
         for n in range(2):
             warm_bank = psum.tile([P, N], F32, name="warm_bank", tag="work", bufs=5)
@@ -313,8 +313,6 @@ def tile_attend_gat_exp_c_kernel(tc, qT, cT, doT, rw, qm, dom, offs, out):
         def quantize_half(name, g, bf, slots):
             quantize(moving[name, g], E4M3 if name == "pw" else E5M2, bf.rearrange("p i t -> p (i t)"), slots)
 
-        warm_bank = psum.tile([P, N], F32, name="warm_bank", tag="gate_bank")
-        matmul(warm_bank[:], c_mx, E4M3, slice(0, P), c_mx, E4M3, True, True)
         quantize(ds0_dom, E5M2, dom0[:].rearrange("p g d j -> p (g d j)"), slice(N, wide))
         dom0 = part(ds0_dom, N, HALF)
         warm_bank = psum.tile([P, N], F32, name="warm_bank", tag="work", bufs=5)
@@ -335,9 +333,9 @@ def tile_attend_gat_exp_c_kernel(tc, qT, cT, doT, rw, qm, dom, offs, out):
 
         sums = copy_sums(first_bank, HALF)
         scatter(0, first, sums)
-        later = keep.tile([P, 5, GROUPS, P, PACK], BF16, name="later_bf", align_bytes=64, tag="ds1_second")
-        dom1 = right_cast("dom", 1, "S", bf=later[:, 0])
-        qm1 = later[:, 1]
+        dom1 = right_cast("dom", 1, "S", tag="pw1_bf")
+        later = keep.tile([P, 4, GROUPS, P, PACK], BF16, name="later_bf", align_bytes=64, tag="ds1_second")
+        qm1 = later[:, 0]
         shared_cast(1, qm1)
         sums = copy_sums(second_bank, HALF)
         dom1 = right_quantize("dom", 1, E5M2, dom1)
@@ -345,7 +343,7 @@ def tile_attend_gat_exp_c_kernel(tc, qT, cT, doT, rw, qm, dom, offs, out):
         bank = products(tile_passes(dom1, qm1_mx))
         scatter(0, second, sums)
         store(0)
-        dom2 = right_cast("dom", 2, "S", bf=later[:, 2])
+        dom2 = right_cast("dom", 2, "S", bf=later[:, 1])
         shared_cast(2, qm1)
         sums = copy_sums(bank, N)
         dom2 = right_quantize("dom", 2, E5M2, dom2)
@@ -353,8 +351,8 @@ def tile_attend_gat_exp_c_kernel(tc, qT, cT, doT, rw, qm, dom, offs, out):
         bank = products(tile_passes(dom2, qm2_mx))
         scatter(1, slice(0, N), sums)
         store(1)
-        dom3 = right_cast("dom", 3, "S", bf=later[:, 3])
-        qm3 = right_cast("qm", 3, "S", bf=later[:, 4])
+        dom3 = right_cast("dom", 3, "S", bf=later[:, 2])
+        qm3 = right_cast("qm", 3, "S", bf=later[:, 3])
         sums = copy_sums(bank, N)
         bank = products(tile_passes(right_quantize("dom", 3, E5M2, dom3), right_quantize("qm", 3, E4M3, qm3)))
         scatter(2, slice(0, N), sums)

@@ -315,8 +315,6 @@ def tile_attend_gat_exp_c_kernel(tc, qT, cT, doT, rw, qm, dom, offs, out):
 
         quantize(ds0_dom, E5M2, dom0[:].rearrange("p g d j -> p (g d j)"), slice(N, wide))
         dom0 = part(ds0_dom, N, HALF)
-        warm_bank = psum.tile([P, N], F32, name="warm_bank", tag="work", bufs=5)
-        matmul(warm_bank[:], dom0, E5M2, slice(0, P), c_mx, E4M3, True, True)
         quantize_half("pw", 1, pw1[:, first], first)
         quantize(pw0_qm, E4M3, qm0[:].rearrange("p g d j -> p (g d j)"), slice(N, wide))
         qm0 = part(pw0_qm, N, HALF)

@@ -26,7 +26,7 @@ HALF = K_PASS // 2
 WINDOWS = 3
 M_LOADS = ((0, 1), (1, 2), (2, 4))
 PAIRS = ((0, 2), (2, PACK))
-LATE0, G1, EARLY, MIDDLE, LAST = 128, 216, 96, 96, 128
+LATE0, G1, EARLY, MIDDLE, LAST, CAST_G = 128, 216, 96, 96, 128, 56
 
 
 def tile_attend_gat_exp_c_kernel(tc, qT, cT, doT, rw, qm, dom, offs, out):
@@ -251,12 +251,12 @@ def tile_attend_gat_exp_c_kernel(tc, qT, cT, doT, rw, qm, dom, offs, out):
             second_queue.dma_start(out=out[dt * P : (dt + 1) * P, T // 2 :], in_=window[:, T // 2 :])
 
         def shared_cast(dt, bf):
-            for g, (engine, run) in enumerate((("S", 2), ("G", 4))):
-                copy_on(
-                    engine,
-                    bf[:, g].rearrange("p (c i) j -> p c j i", i=run),
-                    right_raw["qm", dt][:, g].rearrange("p j (c i) -> p c j i", i=run),
-                )
+            copy_on("G", bf[:, :, :CAST_G, :], right_raw["qm", dt][:, :, :, :CAST_G].rearrange("p g j d -> p g d j"))
+            copy_on(
+                "S",
+                bf[:, :, CAST_G:, :].rearrange("p g (c i) j -> p g c j i", i=2),
+                right_raw["qm", dt][:, :, :, CAST_G:].rearrange("p g j (c i) -> p g c j i", i=2),
+            )
 
         for n in range(2):
             warm_bank = psum.tile([P, N], F32, name="warm_bank", tag="work", bufs=5)
@@ -292,7 +292,7 @@ def tile_attend_gat_exp_c_kernel(tc, qT, cT, doT, rw, qm, dom, offs, out):
         left_quantize("do", 1, E5M2, PAIRS[1:])
         interleave_grads(ds0_bf, ds0, "V", slice(N - LAST, N))
         ds1 = keep.tile([P, PACK, N], BF16, name="ds1", align_bytes=64, tag="do_raw11")
-        score_grads(1, by_slot=ds1)
+        score_grads(1, by_slot=ds1, warm=(3,))
         gated_on_gpsimd(0, pw0[:, :LATE0], slice(0, LATE0))
         dom0 = right_cast("dom", 0, "S")
         qm0 = right_cast("qm", 0, "S")
@@ -313,6 +313,8 @@ def tile_attend_gat_exp_c_kernel(tc, qT, cT, doT, rw, qm, dom, offs, out):
         def quantize_half(name, g, bf, slots):
             quantize(moving[name, g], E4M3 if name == "pw" else E5M2, bf.rearrange("p i t -> p (i t)"), slots)
 
+        warm_bank = psum.tile([P, N], F32, name="warm_bank", tag="gate_bank")
+        matmul(warm_bank[:], c_mx, E4M3, slice(0, P), c_mx, E4M3, True, True)
         quantize(ds0_dom, E5M2, dom0[:].rearrange("p g d j -> p (g d j)"), slice(N, wide))
         dom0 = part(ds0_dom, N, HALF)
         quantize_half("pw", 1, pw1[:, first], first)

@@ -26,7 +26,7 @@ HALF = K_PASS // 2
 WINDOWS = 3
 M_LOADS = ((0, 1), (1, 2), (2, 4))
 PAIRS = ((0, 2), (2, PACK))
-LATE0, G1, EARLY, MIDDLE, LAST, CAST_G = 128, 216, 96, 96, 128, 56
+LATE0, G1, EARLY, MIDDLE, LAST, CAST_G = 128, 216, 96, 96, 128, 64
 
 
 def tile_attend_gat_exp_c_kernel(tc, qT, cT, doT, rw, qm, dom, offs, out):
@@ -222,8 +222,8 @@ def tile_attend_gat_exp_c_kernel(tc, qT, cT, doT, rw, qm, dom, offs, out):
             quantize(mx, fmt, bf[:].rearrange("p g d j -> p (g d j)"))
             return mx
 
-        def products(passes):
-            bank = psum.tile([P, N], F32, name="out_bank", tag="work", bufs=5)
+        def products(passes, tag="work", bufs=5):
+            bank = psum.tile([P, N], F32, name="out_bank", tag=tag, bufs=bufs)
             for n, operands in enumerate(passes):
                 matmul(bank[:], *operands, n == 0, n == len(passes) - 1)
             return bank
@@ -324,14 +324,14 @@ def tile_attend_gat_exp_c_kernel(tc, qT, cT, doT, rw, qm, dom, offs, out):
         quantize_half("ds", 0, ds0_bf[:, first], first)
         quantize_half("ds", 1, ds1_first[:], first)
         passes = tile_passes(dom0, qm0, HALF)
-        first_bank = products([passes[1], passes[0]] + passes[2:])
+        first_bank = products([passes[1], passes[0]] + passes[2:], "gate_bank", 1)
         quantize_half("pw", 0, pw0[:, second], second)
         quantize_half("pw", 1, pw1[:, second], second)
         quantize_half("ds", 0, ds0_bf[:, second], second)
         quantize_half("ds", 1, ds1_second[:], second)
-        second_bank = products(tile_passes(dom0, qm0))
 
         sums = copy_sums(first_bank, HALF)
+        second_bank = products(tile_passes(dom0, qm0), "gate_bank", 1)
         scatter(0, first, sums)
         dom1 = right_cast("dom", 1, "S", tag="pw1_bf")
         later = keep.tile([P, 4, GROUPS, P, PACK], BF16, name="later_bf", align_bytes=64, tag="ds1_second")

from contextlib import ExitStack

import concourse.mybir as mybir
from concourse.masks import make_identity

N, T, D, R = 512, 2048, 512, 1024
FLOPS = 4 * 2 * R * N * D

F32 = mybir.dt.float32
BF16 = mybir.dt.bfloat16
U32 = mybir.dt.uint32
U16 = mybir.dt.uint16
U8 = mybir.dt.uint8
E4M3 = mybir.dt.float8_e4m3fn_x4
E5M2 = mybir.dt.float8_e5m2_x4
MULT = mybir.AluOpType.mult
ADD = mybir.AluOpType.add
EXP = mybir.ActivationFunctionType.Exp

P = 128
PACK = 4
K_PASS = P * PACK
GROUPS = R // K_PASS
D_TILES = D // P
HALF = K_PASS // 2
WINDOWS = 3
M_LOADS = ((0, 1), (1, 2), (2, 4))
PAIRS = ((0, 2), (2, PACK))
LATE0, G1, EARLY, MIDDLE, LAST, CAST_G = 128, 216, 96, 96, 128, 64


def tile_attend_gat_exp_c_kernel(tc, qT, cT, doT, rw, qm, dom, offs, out):
    nc = tc.nc

    def copy_on(engine, dst, src):
        if engine == "V":
            nc.vector.tensor_copy(out=dst, in_=src)
        elif engine == "G":
            nc.gpsimd.tensor_scalar(out=dst, in0=src, scalar1=1.0, scalar2=0.0, op0=MULT, op1=ADD)
        else:
            nc.scalar.copy(out=dst, in_=src)

    with ExitStack() as ctx:
        keep = ctx.enter_context(tc.tile_pool(name="keep", bufs=1))
        ring = ctx.enter_context(tc.tile_pool(name="ring", bufs=2))
        psum = ctx.enter_context(tc.psum_pool(name="psum", bufs=1))

        def mx_tiles(name, width, codes=None):
            if codes is None:
                codes = keep.tile([P, width], U32, name=name + "_codes", align_bytes=64)
            scales = keep.tile([P, width], U8, name=name + "_scales", align_bytes=64)
            return codes, scales

        def quantize(mx, fmt, src, cols=slice(None)):
            codes, scales = mx
            nc.vector.quantize_mx(out=codes[:, cols].bitcast(fmt), scales=scales[:, cols], in_=src)

        def matmul(dst, lhs, lhs_fmt, lhs_cols, rhs, rhs_fmt, start, stop):
            nc.tensor.matmul_mx(
                out=dst,
                lhsT=lhs[0][:, lhs_cols].bitcast(lhs_fmt),
                lhsT_scale=lhs[1][:, lhs_cols],
                rhs=rhs[0][:].bitcast(rhs_fmt),
                rhs_scale=rhs[1][:],
                start=start,
                stop=stop,
            )

        gate_rows = keep.tile([P, K_PASS], F32, name="gate_rows")
        nc.gpsimd.memset(gate_rows[:], 0.0)

        c_rows = cT.rearrange("(p j) x -> p j x", j=PACK)
        planes = []
        for j in range(PACK):
            plane = keep.tile([P, T], F32, name="plane%d" % j)
            nc.sync.dma_start(out=plane[:], in_=c_rows[:, j, :])
            planes.append(plane)
            if j == 0:
                offsets = keep.tile([P, N // 16], U16, name="offsets")
                nc.sync.dma_start(offsets[:], offs)
                nc.sync.dma_start(out=gate_rows[:GROUPS, :], in_=rw[0].rearrange("(g r) o -> g (r o)", g=GROUPS))

        identity = keep.tile([P, P], F32, name="identity")
        make_identity(nc, identity[:])
        gate_bank = psum.tile([P, PACK, P], F32, name="gate_bank")
        for t in range(PACK):
            nc.tensor.transpose(gate_bank[:, t], gate_rows[:, t::PACK], identity[:])
        bank_gates = gate_bank[:, :, :GROUPS].rearrange("p t g -> p g t")
        gates = keep.tile([P, GROUPS, PACK], F32, name="gates", align_bytes=64)
        nc.scalar.copy(out=gates[:], in_=bank_gates)

        left_raw = {}
        for g in range(GROUPS):
            for name, src in (("q", qT), ("do", doT)):
                rows = src[0].rearrange("(p j) r -> p j r", j=PACK)
                for h in range(2):
                    raw = keep.tile([P, PACK, HALF], F32, name="%s_raw%d%d" % (name, g, h), align_bytes=64)
                    r0 = g * K_PASS + h * HALF
                    nc.sync.dma_start(out=raw[:], in_=rows[:, :, r0 : r0 + HALF])
                    left_raw[name, g, h] = raw

        right_raw = {}
        for lo, hi in M_LOADS:
            for name, src in (("dom", dom), ("qm", qm)):
                raw = keep.tile([P, GROUPS, PACK, (hi - lo) * P], F32, name="%s_raw%d" % (name, lo), align_bytes=64)
                for g in range(GROUPS):
                    rows = src[0, g * K_PASS : (g + 1) * K_PASS, :].rearrange("(p j) d -> p j d", j=PACK)
                    nc.sync.dma_start(out=raw[:, g], in_=rows[:, :, lo * P : hi * P])
                for dt in range(lo, hi):
                    right_raw[name, dt] = raw[:, :, :, (dt - lo) * P : (dt - lo + 1) * P]

        windows = []
        for dt in range(WINDOWS):
            window = keep.tile([P, T], F32, name="window%d" % dt)
            nc.gpsimd.memset(window[:], 0.0)
            windows.append(window)

        c_bf = keep.tile([P, N, PACK], BF16, name="c_bf", align_bytes=64)
        for j in range(PACK - 1):
            nc.vector.tensor_copy(out=c_bf[:, :, j], in_=planes[j][:].indirect(offsets[:]))
        for h in range(2):
            listed = offsets[:, h * HALF // 16 : (h + 1) * HALF // 16]
            nc.vector.tensor_copy(out=c_bf[:, h * HALF : (h + 1) * HALF, PACK - 1], in_=planes[PACK - 1][:].indirect(listed))
        def part(mx, start, width):
            return mx[0][:, start : start + width], mx[1][:, start : start + width]

        pw1_c = mx_tiles("pw1_c", 2 * N)
        c_mx = part(pw1_c, N, N)
        for h in range(2):
            cols = slice(h * HALF, (h + 1) * HALF)
            quantize(c_mx, E4M3, c_bf[:, cols, :].rearrange("p i j -> p (i j)"), cols)

        ds1_do = mx_tiles("ds1_do", 2 * N)
        left_mx = {("do", 1): part(ds1_do, N, K_PASS)}

        left_bf = {}

        def left_cast(name, g, h, engine, tag="", cut=""):
            if (name, g) not in left_bf:
                left_bf[name, g] = keep.tile([P, PACK, P, PACK], BF16, name="left_bf", align_bytes=64, tag=tag or "left_%s%d" % (name, g))
            m = slice(h * (P // 2), (h + 1) * (P // 2))
            dst = left_bf[name, g][:, :, m, :].rearrange("p t m j -> p m j t")
            src = left_raw[name, g, h][:].rearrange("p j (m t) -> p m j t", t=PACK)
            if cut:
                for lo, pair_engine in zip((0, 2), cut):
                    copy_on(pair_engine, dst[:, :, :, lo : lo + 2], src[:, :, :, lo : lo + 2])
            else:
                copy_on(engine, dst.rearrange("p m j (u e) -> p u m j e", e=2), src.rearrange("p m j (u e) -> p u m j e", e=2))

        def left_quantize(name, g, fmt, runs=((0, 1), (1, 2), (2, PACK))):
            bf = left_bf[name, g]
            if (name, g) not in left_mx:
                left_mx[name, g] = mx_tiles("%s%d" % (name, g), K_PASS)
            for lo, hi in runs:
                quantize(left_mx[name, g], fmt, bf[:, lo:hi].rearrange("p t m j -> p (t m j)"), slice(lo * P, hi * P))

        weights = {}

        def scores(g, places=range(PACK)):
            if g not in weights:
                weights[g] = keep.tile([P, PACK, N], F32, name="p32_%d" % g, align_bytes=64)
            for t in places:
                bank = psum.tile([P, N], F32, name="a_bank", tag="work", bufs=5)
                matmul(bank[:], left_mx["q", g], E4M3, slice(t * P, (t + 1) * P), c_mx, E4M3, True, True)
                nc.scalar.activation(out=weights[g][:, t, :], in_=bank[:], func=EXP)

        moving = {}

        def gated_on_gpsimd(g, bf, slots):
            width = slots.stop - slots.start
            nc.gpsimd.tensor_tensor(
                out=bf.rearrange("p (c i) t -> p c t i", i=4),
                in0=weights[g][:, :, slots].rearrange("p t (c i) -> p c t i", i=4),
                in1=gates[:, g, :].unsqueeze(1).unsqueeze(3).to_broadcast([P, width // 4, PACK, 4]),
                op=MULT,
            )

        def gated_on_vector(g, bf, slots):
            width = slots.stop - slots.start
            nc.vector.tensor_tensor(
                out=bf.rearrange("p (c i) t -> p c t i", i=2),
                in0=weights[g][:, :, slots].rearrange("p t (c i) -> p c t i", i=2),
                in1=bank_gates[:, g, :].unsqueeze(1).unsqueeze(3).to_broadcast([P, width // 2, PACK, 2]),
                op=MULT,
            )

        def score_grads(g, places=range(PACK), by_slot=None, warm=()):
            if by_slot is None:
                by_slot = ring.tile([P, PACK, N], BF16, name="ds_by_slot")
            for t in places:
                if g == 0 or t < 2:
                    bank = psum.tile([P, N], F32, name="dp_bank", tag="dp", bufs=2)
                else:
                    bank = psum.tile([P, N], F32, name="dp_late_bank", tag="work", bufs=5)
                matmul(bank[:], left_mx["do", g], E5M2, slice(t * P, (t + 1) * P), c_mx, E4M3, True, True)
                nc.vector.scalar_tensor_tensor(
                    out=by_slot[:, t, :], in0=bank[:], scalar=gates[:, g, t : t + 1], in1=weights[g][:, t, :], op0=MULT, op1=MULT
                )
                if t in warm:
                    matmul(bank[:], left_mx["do", g], E5M2, slice(t * P, (t + 1) * P), c_mx, E4M3, True, True)
            return by_slot

        def interleave_grads(bf, by_slot, engine, slots):
            copy_on(
                engine,
                bf[:, slots, :].rearrange("p (c i) t -> p c t i", i=4),
                by_slot[:, :, slots].rearrange("p t (c i) -> p c t i", i=4),
            )

        def right_cast(name, dt, engine, tag="", bf=None):
            if bf is None:
                bf = keep.tile([P, GROUPS, P, PACK], BF16, name="%s_bf%d" % (name, dt), align_bytes=64, tag=tag)
            copy_on(
                engine,
                bf[:].rearrange("p g (c i) j -> p g c j i", i=2),
                right_raw[name, dt].rearrange("p g j (c i) -> p g c j i", i=2),
            )
            return bf

        def right_quantize(name, dt, fmt, bf, codes=None):
            mx = mx_tiles("%s_t%d" % (name, dt), GROUPS * P, codes)
            quantize(mx, fmt, bf[:].rearrange("p g d j -> p (g d j)"))
            return mx

        def products(passes, tag="work", bufs=5):
            bank = psum.tile([P, N], F32, name="out_bank", tag=tag, bufs=bufs)
            for n, operands in enumerate(passes):
                matmul(bank[:], *operands, n == 0, n == len(passes) - 1)
            return bank

        def tile_passes(dom_mx, qm_mx, shift=0):
            passes = []
            for lhs, lhs_fmt, name, rhs_fmt in ((dom_mx, E5M2, "pw", E4M3), (qm_mx, E4M3, "ds", E5M2)):
                for g in range(GROUPS):
                    passes.append((lhs, lhs_fmt, slice(g * P, (g + 1) * P), part(moving[name, g], shift, N), rhs_fmt))
            return passes

        def copy_sums(bank, width):
            sums = ring.tile([P, width], F32, name="sums")
            nc.scalar.copy(out=sums[:], in_=bank[:, :width])
            return sums

        def scatter(dt, slots, sums):
            listed = offsets[:, slots.start // 16 : slots.stop // 16]
            nc.vector.tensor_copy(out=windows[dt % WINDOWS][:].indirect(listed), in_=sums[:])

        def store(dt):
            window = windows[dt % WINDOWS]
            second_queue = nc.scalar if dt == D_TILES - 1 else nc.sync
            nc.sync.dma_start(out=out[dt * P : (dt + 1) * P, : T // 2], in_=window[:, : T // 2])
            second_queue.dma_start(out=out[dt * P : (dt + 1) * P, T // 2 :], in_=window[:, T // 2 :])

        def shared_cast(dt, bf):
            copy_on("G", bf[:, :, :CAST_G, :], right_raw["qm", dt][:, :, :, :CAST_G].rearrange("p g j d -> p g d j"))
            copy_on(
                "S",
                bf[:, :, CAST_G:, :].rearrange("p g (c i) j -> p g c j i", i=2),
                right_raw["qm", dt][:, :, :, CAST_G:].rearrange("p g j (c i) -> p g c j i", i=2),
            )

        for n in range(2):
            warm_bank = psum.tile([P, N], F32, name="warm_bank", tag="work", bufs=5)
            matmul(warm_bank[:], c_mx, E4M3, slice(n * P, (n + 1) * P), c_mx, E4M3, True, True)
        left_cast("q", 0, 0, "S")
        left_cast("q", 0, 1, "V", cut="VS")
        left_quantize("q", 0, E4M3)
        scores(0)
        left_cast("do", 0, 0, "V")
        left_cast("do", 0, 1, "V", cut="VV")
        left_quantize("do", 0, E5M2)
        pw0_at = PACK * N - LAST
        group0 = keep.tile([P, pw0_at + PACK * N], BF16, name="group0", align_bytes=64, tag="left_do0")
        ds0 = group0[:, : PACK * N].rearrange("p (t i) -> p t i", t=PACK)
        pw0 = group0[:, pw0_at:].rearrange("p (i t) -> p i t", t=PACK)
        score_grads(0, by_slot=ds0, warm=())
        pw1 = keep.tile([P, N, PACK], BF16, name="pw1_bf", align_bytes=64)
        gated_on_gpsimd(0, pw0[:, HALF:], slice(HALF, N))
        gated_on_vector(0, pw0[:, LATE0:HALF], slice(LATE0, HALF))
        left_cast("q", 1, 0, "S")
        left_cast("q", 1, 1, "S")
        shared = keep.tile([P, 2 * N - LAST, PACK], BF16, name="shared", align_bytes=64, tag="q_raw11")
        ds0_bf = shared[:, :N]
        left_bf["do", 1] = shared[:, N - LAST :].rearrange("p (t m) j -> p t m j", t=PACK)
        left_cast("do", 1, 0, "S")
        left_quantize("q", 1, E4M3, PAIRS[:1])
        left_quantize("q", 1, E4M3, PAIRS[1:])
        interleave_grads(ds0_bf, ds0, "V", slice(N - LAST - MIDDLE, N - LAST))
        left_cast("do", 1, 1, "V", cut="VV")
        interleave_grads(ds0_bf, ds0, "S", slice(N - LAST - MIDDLE - EARLY, N - LAST - MIDDLE))
        scores(1)
        left_quantize("do", 1, E5M2, PAIRS[:1])
        left_quantize("do", 1, E5M2, PAIRS[1:])
        interleave_grads(ds0_bf, ds0, "V", slice(N - LAST, N))
        ds1 = keep.tile([P, PACK, N], BF16, name="ds1", align_bytes=64, tag="do_raw11")
        score_grads(1, by_slot=ds1, warm=(3,))
        gated_on_gpsimd(0, pw0[:, :LATE0], slice(0, LATE0))
        dom0 = right_cast("dom", 0, "S")
        qm0 = right_cast("qm", 0, "S")
        first, second = slice(HALF, N), slice(0, HALF)
        ds1_first = keep.tile([P, HALF, PACK], BF16, name="ds1_first", align_bytes=64)
        ds1_second = keep.tile([P, HALF, PACK], BF16, name="ds1_second", align_bytes=64)
        interleave_grads(ds1_first, ds1[:, :, first], "S", slice(0, HALF))
        interleave_grads(ds0_bf, ds0, "S", slice(0, N - LAST - MIDDLE - EARLY))
        interleave_grads(ds1_second, ds1[:, :, second], "S", slice(0, HALF))
        gated_on_gpsimd(1, pw1[:, N - G1 :], slice(N - G1, N))
        gated_on_vector(1, pw1[:, : N - G1], slice(0, N - G1))
        wide = N + HALF
        group0_codes = keep.tile([P, 2 * wide], U32, name="group0_codes", align_bytes=64, tag="gates")
        pw0_qm = mx_tiles("pw0_qm", wide, group0_codes[:, :wide])
        ds0_dom = mx_tiles("ds0_dom", wide, group0_codes[:, wide:])
        moving.update({("pw", 0): pw0_qm, ("pw", 1): pw1_c, ("ds", 0): ds0_dom, ("ds", 1): ds1_do})

        def quantize_half(name, g, bf, slots):
            quantize(moving[name, g], E4M3 if name == "pw" else E5M2, bf.rearrange("p i t -> p (i t)"), slots)

        warm_bank = psum.tile([P, N], F32, name="warm_bank", tag="gate_bank")
        matmul(warm_bank[:], c_mx, E4M3, slice(0, P), c_mx, E4M3, True, True)
        quantize(ds0_dom, E5M2, dom0[:].rearrange("p g d j -> p (g d j)"), slice(N, wide))
        dom0 = part(ds0_dom, N, HALF)
        quantize_half("pw", 1, pw1[:, first], first)
        quantize(pw0_qm, E4M3, qm0[:].rearrange("p g d j -> p (g d j)"), slice(N, wide))
        qm0 = part(pw0_qm, N, HALF)
        quantize_half("pw", 0, pw0[:, first], first)
        quantize_half("ds", 0, ds0_bf[:, first], first)
        quantize_half("ds", 1, ds1_first[:], first)
        passes = tile_passes(dom0, qm0, HALF)
        first_bank = products([passes[1], passes[0]] + passes[2:], "gate_bank", 1)
        quantize_half("pw", 0, pw0[:, second], second)
        quantize_half("pw", 1, pw1[:, second], second)
        quantize_half("ds", 0, ds0_bf[:, second], second)
        quantize_half("ds", 1, ds1_second[:], second)

        sums = copy_sums(first_bank, HALF)
        second_bank = products(tile_passes(dom0, qm0), "gate_bank", 1)
        scatter(0, first, sums)
        dom1 = right_cast("dom", 1, "S", tag="pw1_bf")
        later = keep.tile([P, 4, GROUPS, P, PACK], BF16, name="later_bf", align_bytes=64, tag="ds1_second")
        qm1 = later[:, 0]
        shared_cast(1, qm1)
        sums = copy_sums(second_bank, HALF)
        dom1 = right_quantize("dom", 1, E5M2, dom1)
        qm1_mx = right_quantize("qm", 1, E4M3, qm1)
        bank = products(tile_passes(dom1, qm1_mx))
        scatter(0, second, sums)
        store(0)
        dom2 = right_cast("dom", 2, "S", bf=later[:, 1])
        shared_cast(2, qm1)
        sums = copy_sums(bank, N)
        dom2 = right_quantize("dom", 2, E5M2, dom2)
        qm2_mx = right_quantize("qm", 2, E4M3, qm1)
        bank = products(tile_passes(dom2, qm2_mx))
        scatter(1, slice(0, N), sums)
        store(1)
        dom3 = right_cast("dom", 3, "S", bf=later[:, 2])
        qm3 = right_cast("qm", 3, "S", bf=later[:, 3])
        sums = copy_sums(bank, N)
        bank = products(tile_passes(right_quantize("dom", 3, E5M2, dom3), right_quantize("qm", 3, E4M3, qm3)))
        scatter(2, slice(0, N), sums)
        store(2)
        scatter(3, slice(0, N), copy_sums(bank, N))
        store(3)
